import numpy as np, ml_dtypes
CORES = [40,41,42,43,44,45,46,47]
N = 8
import mx_ref
BF = ml_dtypes.bfloat16
def entries(a):
    return np.ascontiguousarray(a.T).reshape(-1)
def table(e):
    return np.ascontiguousarray(np.reshape(e, (-1, 16)).T).astype(np.int32)
def cols(t, e):
    v = np.concatenate([t.reshape(128, -1, 4), np.zeros((128, 1, 4), BF)], axis=1)
    return np.ascontiguousarray(v[:, e]).reshape(128, -1)
def decode(q):
    o = []
    for b in range(4):
        e = np.zeros((128, 128, 4), np.float32); e[np.arange(128), np.arange(128), b] = 1
        o.append(mx_ref.matmul(mx_ref.quantize(e.reshape(128, 512).astype(BF)), q))
    return np.stack(o, axis=2).reshape(128, -1)
def f(rng, *shape):
    return mx_ref.flush((rng.standard_normal(shape, dtype=np.float32) * np.exp2(rng.integers(-2, 3, shape[:-1] + (1,)))).astype(BF))
def wide(rng, *shape, cols=0):
    v = rng.standard_normal(shape, dtype=np.float32) * np.exp2(rng.integers(-12, 13, shape)).astype(np.float32)
    if cols: v *= np.repeat(np.exp2(rng.integers(-cols, cols + 1, shape[:-2] + (1, shape[-1] // 4))) * (rng.random(shape[:-2] + (1, shape[-1] // 4)) > 0.0625), 4, axis=-1).astype(np.float32)
    return mx_ref.flush(v.astype(BF))
TC, T, CAPP, O = 512, 256, 32, 2
def lists(rng, n, front=False):
    a = np.full((N, N, CAPP), -1)
    b = np.full((N, N, CAPP), -1)
    for s in range(N):
        for d in range(N):
            k = rng.permutation(CAPP)[:n[s, d]]
            a[s, d, k] = rng.integers(0, T, len(k)); b[d, s, k] = 0
    for d in range(N):
        used = b[d] == 0; u = int(used.sum())
        b[d][used] = np.arange(u) if front else rng.permutation(TC)[:u]
    return {"snd": np.stack([table(a[s]) for s in range(N)]), "plc": np.stack([table(b[d]) for d in range(N)])}
def tiles(rng):
    return {"kc": f(rng, N, 128, 4 * TC), "x": f(rng, N, 128, 4 * T), "qw": f(rng, N, 128, 512 * O)}
def setup_inputs(rng):
    return {**tiles(rng), **lists(rng, rng.integers(0, CAPP + 1, (N, N)))}
def setup_inputs_full(rng):
    return {**tiles(rng), **lists(rng, np.full((N, N), CAPP))}
def setup_inputs_few(rng):
    n = rng.integers(0, 3, (N, N))
    for d in range(N):
        o = rng.permutation([s for s in range(N) if s != d])
        n[o[0], d] = 0; n[o[1], d] = 1
    n[:, rng.integers(0, N)] = 0
    return {**tiles(rng), **lists(rng, n)}
def setup_inputs_front(rng):
    return {**tiles(rng), **lists(rng, rng.integers(1, CAPP + 1, (N, N)), front=True)}
def setup_inputs_own(rng):
    n = rng.integers(0, 3, (N, N)); n[np.arange(N), np.arange(N)] = CAPP
    return {**tiles(rng), **lists(rng, n)}
def setup_inputs_spread(rng):
    d = setup_inputs(rng); d["x"] = wide(rng, N, 128, 4 * T, cols=8); d["kc"] = wide(rng, N, 128, 4 * TC); return d
def check_inputs(d):
    b = []
    a = np.stack([entries(d["snd"][r]).reshape(N, CAPP) for r in range(N)])
    p = np.stack([entries(d["plc"][r]).reshape(N, CAPP) for r in range(N)])
    if a.min() < -1 or a.max() >= T: b.append("snd")
    if p.min() < -1 or p.max() >= TC: b.append("plc")
    if ((a.transpose(1, 0, 2) == -1) != (p == -1)).any(): b.append("plc is -1 exactly where the slot is empty")
    for r in range(N):
        v = p[r][p[r] != -1].tolist()
        if len(set(v)) != len(v): b.append("plc differs"); break
    return b
def reference(kc, x, qw, snd, plc):
    y = np.zeros((N, 128, O * TC), np.float32)
    for r in range(N):
        sent = np.concatenate([cols(x[s], entries(snd[s])[r * CAPP:(r + 1) * CAPP]) for s in range(N)], axis=1)
        got = decode(mx_ref.quantize(sent)).astype(BF).reshape(128, N * CAPP, 4)
        p = entries(plc[r]); used = p >= 0
        c = kc[r].reshape(128, TC, 4).copy()
        c[:, p[used]] = got[:, used]
        c = mx_ref.quantize(np.ascontiguousarray(c).reshape(128, 4 * TC))
        for o in range(O):
            y[r][:, TC * o:TC * o + TC] = mx_ref.matmul(mx_ref.quantize(np.ascontiguousarray(qw[r][:, 512 * o:512 * o + 512])), c)
    return {"y": y}

@@ -1,0 +1,242 @@
+from concourse.bass import DstId, RemoteDMATransfer
+from concourse.mybir import dt, AluOpType, ActivationFunctionType
+
+N, CAPP, XC, HC, TC = 8, 32, 256, 128, 512
+HALF = N // 2
+ARR = (N - 1) * CAPP
+VI = TC + 32
+VW = VI + 368
+FAR = 1024
+YP = ((0, 192), (192, 320))
+CALLS = ((False, (0,)), (False, (1,)), (True, (0, 1)))
+VSTEPS = "e0 e1 t x0 e2 e3 c00 x1 c02 o c10 c12 p00 p02 p10 h0 p12 h1"
+ASTEPS = "c01 c03 c11 c13 p01 p03 p11 p13 f j"
+
+
+def _buffers():
+    b = {}
+    for dtype, names in (("bfloat16", {"xb": 1024, "kb": 2048, "qb": 1024, "dg": 128, "ez": VI, "xd0": XC, "xd1": XC, "xd2": XC, "xd3": XC, "hb0": 512, "hb1": 512,
+                                       "vals": XC, "vl": VW, "tr": VI, "tab": 128, "tabt": 128}),
+                         ("int32", {"sl": 16, "pl": 16, "kneg": 16}),
+                         ("uint16", {"so": 16, "po": 16, "inv": 32, "eoff": 2}),
+                         ("float32", {"far": 1, "nk": 16, "pm": 16, "jc": 32, "jt": 32, "sf": 32, "w0": TC + XC, "w1": TC + XC, "y0": TC, "y1": TC})):
+        for k, w in names.items():
+            b[k] = ("sbuf", [128, w], dtype)
+    for q, s, w in (("eq", "es", 512), ("xq", "xs", XC), ("hq0", "hs0", HC), ("hq1", "hs1", HC), ("aq", "asc", ARR), ("kq", "ks", TC), ("wq", "ws", XC)):
+        b[q] = ("sbuf", [128, w], "float8_e4m3fn_x4")
+        b[s] = ("sbuf", [128, w], "uint8")
+    for p in ("pd0", "pd1", "pd2", "pd3", "py0", "py1", "py2", "py3"):
+        b[p] = ("psum", [128, 512], "float32")
+    return b
+
+
+SCRATCH = _buffers()
+SEMAPHORES = ("lx0 lx1 lsnd lplc lqw lkc out arr sent dg far ez0 ez eq0 eq1 eq2 eq3 qx0 qx1 conv hq0 hq1 wq kq0 kq1 tab tabt eoff kneg vals jc jt vinit "
+              "ia ib ic ie it iu inv mo0 mo1 co0 co1 mk00 mk01 mk10 mk11 ck00 ck01 ck10 ck11 ma0 ma1 ca0 ca1 y00 y01 y10 y11 "
+              "m00 m01 m02 m03 m10 m11 m12 m13 c00 c01 c02 c03 c10 c11 c12 c13 g00 g01 g02 g03 g10 g11 g12 g13").split()
+
+
+def send_masks(core, dests, topo):
+    near = [d for d in dests if topo.die(d) == topo.die(core)]
+    far = [d for d in dests if topo.die(d) != topo.die(core)]
+    masks = {}
+    for group, first in ((far, 0), (near, 1)):
+        for k, d in enumerate(group):
+            e = topo.engines(core, d)
+            masks[d] = (1 << e[4 * k + first]) | (1 << e[4 * k + first + 2])
+    return masks
+
+
+def rank_program(g, core, T, topo):
+    rank = T.rank_of(core)
+    if rank is None:
+        return
+    S = T.sem
+    v, a, t, sy = g.vector, g.scalar, g.tensor, g.sync
+    COPY, IDENT = ActivationFunctionType.Copy, ActivationFunctionType.Identity
+    A = AluOpType
+    half, pos = rank // HALF, rank % HALF
+    halves = (1 - half, half)
+
+    def copy(q, out, win, sem):
+        if q is v:
+            v.tensor_copy(out, win).then_inc(S[sem], 1)
+        else:
+            a.activation(out, win, COPY).then_inc(S[sem], 1)
+
+    for h in range(2):
+        sy.dma_start(T.xb[:, 512 * h:512 * h + 512], T.x[:, 512 * h:512 * h + 512]).then_inc(S["lx%d" % h], 16)
+    for k in range(8):
+        a.dma_start(T.sl[16 * k:16 * k + 16, :], T.snd[:, :]).then_inc(S.lsnd, 16)
+    for k in range(8):
+        sy.dma_start(T.pl[16 * k:16 * k + 16, :], T.plc[:, :]).then_inc(S.lplc, 16)
+    sy.dma_start(T.qb[:], T.qw[:, :]).then_inc(S.lqw, 16)
+    sy.dma_start(T.kb[:], T.kc[:, :]).then_inc(S.lkc, 16)
+
+    g.iota(T.dg[:], [[-1, 128]], 0, 1, allow_small_or_imprecise_dtypes=True).then_inc(S.dg, 1)
+    v.memset(T.ez[:], 0.0).then_inc(S.ez0, 1)
+    v.wait_ge(S.dg, 1)
+    v.wait_ge(S.ez0, 1)
+    v.tensor_scalar(T.ez[:, 3:515:4], T.dg[:], 0.0, None, A.is_equal).then_inc(S.ez, 1)
+    g.iota(T.tab[:, 0:64], [[256, 2], [-16, 2], [16, 16]], 16, 0, allow_small_or_imprecise_dtypes=True).then_inc(S.tab, 1)
+    g.iota(T.tab[:, 64:96], [[-16, 2], [0, 16]], 16, 0, allow_small_or_imprecise_dtypes=True).then_inc(S.tab, 1)
+    g.iota(T.tab[:, 96:128], [[0, 2], [1, 16]], 0, 0, allow_small_or_imprecise_dtypes=True).then_inc(S.tab, 1)
+    g.iota(T.far[:], [[0, 1]], FAR, 0, allow_small_or_imprecise_dtypes=True).then_inc(S.far, 1)
+    g.iota(T.jc[:], [[16, 32]], XC, 0, allow_small_or_imprecise_dtypes=True).then_inc(S.jc, 1)
+    g.iota(T.kneg[:], [[-16, 16]], -VI, -1).then_inc(S.kneg, 1)
+    nv = 0
+    for at, n, base in ((HC * halves[0], HC, 0), (HC * half, CAPP * pos, HC), (CAPP * rank, CAPP, ARR),
+                        (CAPP * rank + CAPP, HC - CAPP * pos - CAPP, HC + CAPP * pos)):
+        if n:
+            g.iota(T.vals[:, at:at + n], [[1, n]], base, 0, allow_small_or_imprecise_dtypes=True).then_inc(S.vals, 1)
+            nv += 1
+
+    def quant_e(b):
+        v.wait_ge(S.ez, 1)
+        v.quantize_mx(T.eq[:, 128 * b:128 * b + 128], T.es[:, 128 * b:128 * b + 128], T.ez[:, 3 - b:3 - b + 512]).then_inc(S["eq%d" % b], 1)
+
+    def quant_x(h):
+        v.wait_ge(S["lx%d" % h], 16)
+        v.quantize_mx(T.xq[:, HC * h:HC * h + HC], T.xs[:, HC * h:HC * h + HC],
+                      T.xb[:, 512 * h:512 * h + 512]).then_inc(S["qx%d" % h], 1)
+
+    def tables():
+        v.wait_ge(S.tab, 3)
+        v.transpose(T.tabt[:], T.tab[:]).then_inc(S.tabt, 1)
+
+    def unpack(q, h, b):
+        q.wait_ge(S["m%d%d" % (h, b)], 1)
+        copy(q, T["xd%d" % b][:, HC * h:HC * h + HC], T[("pd%d", "py%d")[h] % b][:, 0:HC], "c%d%d" % (h, b))
+
+    def offsets():
+        v.wait_ge(S.lsnd, 128)
+        v.tensor_copy(T.so[:], T.sl[:]).then_inc(S.conv, 1)
+
+    def pick(q, ph, b):
+        q.wait_ge(S.conv, 1)
+        q.wait_ge(S["c0%d" % b], 1)
+        q.wait_ge(S["c1%d" % b], 1)
+        c = 2 * HALF * halves[ph]
+        copy(q, T["hb%d" % ph][:, b:512:4], T["xd%d" % b][:, 0:XC].indirect(T.so[:, c:c + 2 * HALF]), "g%d%d" % (ph, b))
+
+    def quant_h(ph):
+        for b in range(4):
+            v.wait_ge(S["g%d%d" % (ph, b)], 1)
+        v.quantize_mx(T["hq%d" % ph][:], T["hs%d" % ph][:], T["hb%d" % ph][:]).then_inc(S["hq%d" % ph], 1)
+
+    for h in range(2):
+        t.wait_ge(S["qx%d" % h], 1)
+        for b in range(4):
+            t.wait_ge(S["eq%d" % b], 1)
+            t.matmul_mx(T[("pd%d", "py%d")[h] % b][:, 0:HC], T.eq[:, 128 * b:128 * b + 128], T.es[:, 128 * b:128 * b + 128],
+                        T.xq[:, HC * h:HC * h + HC], T.xs[:, HC * h:HC * h + HC], True, True).then_inc(S["m%d%d" % (h, b)], 1)
+    for q, steps in ((v, VSTEPS), (a, ASTEPS)):
+        for w in steps.split():
+            n = [int(c) for c in w[1:]]
+            if w[0] == "e":
+                quant_e(*n)
+            elif w[0] == "t":
+                tables()
+            elif w[0] == "x":
+                quant_x(*n)
+            elif w[0] == "c":
+                unpack(q, *n)
+            elif w[0] == "o":
+                offsets()
+            elif w[0] == "p":
+                pick(q, *n)
+            elif w[0] == "h":
+                quant_h(*n)
+            elif w[0] == "f":
+                a.wait_ge(S.far, 1)
+                a.wait_ge(S.ez, 1)
+                a.activation(T.vl[:, 0:VI], T.ez[:], IDENT, bias=T.far[:, 0:1], scale=0.0).then_inc(S.vinit, 1)
+            else:
+                a.wait_ge(S.tabt, 1)
+                a.wait_ge(S.jc, 1)
+                a.activation(T.jt[:], T.jc[:], IDENT, bias=T.tabt[:, 96:97]).then_inc(S.jt, 1)
+
+    masks = send_masks(core, [c for c in T.cores if c != core], topo)
+    for planes, parts in CALLS:
+        tr = []
+        for ph in parts:
+            g.wait_ge(S["hq%d" % ph], 1)
+            for k in range(HALF):
+                d = HALF * halves[ph] + k
+                if d == rank:
+                    continue
+                dst = T.cores[d]
+                rid, pid = topo.addr(dst)[:2]
+                lo = CAPP * k
+                at = HC * ph + CAPP * (pos - (1 if ph and rank > d else 0))
+                if planes:
+                    src, out = T["hs%d" % ph][:, lo:lo + CAPP], T.asc[:, at:at + CAPP]
+                else:
+                    src, out = T["hq%d" % ph][:, lo:lo + CAPP].bitcast(dt.uint8), T.aq[:, at:at + CAPP].bitcast(dt.uint8)
+                tr.append(RemoteDMATransfer(dst_ids=[DstId(rid=rid, pnc=pid)], dma_engine_mask=masks[dst],
+                                            remote_sem=S.arr, srcs=[src], dsts=[out]))
+        g.remote_dma_fused(tr, local_sem=S.sent)
+
+    v.wait_ge(S.lplc, 128)
+    v.wait_ge(S.kneg, 1)
+    v.tensor_tensor(T.nk[:], T.pl[:], T.kneg[:], A.mult).then_inc(S.ia, 1)
+    v.wait_ge(S.lqw, 16)
+    v.quantize_mx(T.wq[:], T.ws[:], T.qb[:]).then_inc(S.wq, 1)
+    v.wait_ge(S.ia, 1)
+    v.tensor_tensor(T.pm[:], T.nk[:], T.pl[:], A.max).then_inc(S.ib, 1)
+    v.wait_ge(S.lkc, 16)
+    v.quantize_mx(T.kq[:, 0:256], T.ks[:, 0:256], T.kb[:, 0:1024]).then_inc(S.kq0, 1)
+    v.wait_ge(S.ib, 1)
+    v.wait_ge(S.tabt, 1)
+    v.tensor_scalar(T.po[:], T.pm[:], T.tabt[:, 64:65], None, A.add).then_inc(S.ic, 1)
+    v.quantize_mx(T.kq[:, 256:512], T.ks[:, 256:512], T.kb[:, 1024:2048]).then_inc(S.kq1, 1)
+    v.wait_ge(S.ic, 1)
+    v.wait_ge(S.vals, nv)
+    v.wait_ge(S.vinit, 1)
+    v.tensor_copy(T.vl[:, 0:VW].indirect(T.po[:, 0:16]), T.vals[:, 0:XC]).then_inc(S.ie, 1)
+    v.tensor_copy(T.eoff[:], T.tabt[:, 0:64:32]).then_inc(S.eoff, 1)
+    v.wait_ge(S.ie, 1)
+    v.transpose(T.tr[:], T.vl[:, 0:VI]).then_inc(S.it, 1)
+    v.wait_ge(S.it, 1)
+    v.wait_ge(S.eoff, 1)
+    v.wait_ge(S.jt, 1)
+    v.tensor_tensor(T.sf[:], T.tr[:, 0:VI].indirect(T.eoff[:, 0:2]), T.jt[:], A.min).then_inc(S.iu, 1)
+    v.wait_ge(S.iu, 1)
+    v.tensor_copy(T.inv[:], T.sf[:]).then_inc(S.inv, 1)
+
+    def product(bank, o, q, s, n, sem):
+        t.matmul_mx(T[bank][:, 0:n], T.wq[:, 128 * o:128 * o + 128], T.ws[:, 128 * o:128 * o + 128], q, s, True, True).then_inc(S[sem], 1)
+    t.wait_ge(S.wq, 1)
+    for h, bank in ((0, "py%d"), (1, "pd%d")):
+        t.wait_ge(S["kq%d" % h], 1)
+        for o in range(2):
+            t.wait_ge(S["c%d%d" % (1 - h, o)], 1)
+            product(bank % o, o, T.kq[:, 256 * h:256 * h + 256], T.ks[:, 256 * h:256 * h + 256], 256, "mk%d%d" % (h, o))
+            a.wait_ge(S["mk%d%d" % (h, o)], 1)
+            copy(a, T["w%d" % o][:, XC + 256 * h:XC + 256 * h + 256], T[bank % o][:, 0:256], "ck%d%d" % (h, o))
+    for o in range(2):
+        bank = "py%d" % (2 + o)
+        t.wait_ge(S["c1%d" % (2 + o)], 1)
+        product(bank, o, T.hq1[:], T.hs1[:], HC, "mo%d" % o)
+        a.wait_ge(S["mo%d" % o], 1)
+        copy(a, T["w%d" % o][:, ARR:XC], T[bank][:, CAPP * pos:CAPP * pos + CAPP], "co%d" % o)
+
+    t.wait_ge(S.arr, 2 * 2 * (N - 1))
+    for o in range(2):
+        t.wait_ge(S["c0%d" % (2 + o)], 1)
+        product("pd%d" % (2 + o), o, T.aq[:], T.asc[:], ARR, "ma%d" % o)
+
+    for o, q in ((0, v), (1, a)):
+        q.wait_ge(S["ma%d" % o], 1)
+        copy(q, T["w%d" % o][:, 0:ARR], T["pd%d" % (2 + o)][:, 0:ARR], "ca%d" % o)
+        for s in ("co%d", "ck0%d", "ck1%d", "ca%d"):
+            q.wait_ge(S[s % o], 1)
+        q.wait_ge(S.inv, 1)
+        for i, (at, n) in enumerate(YP):
+            copy(q, T["y%d" % o][:, at:at + n], T["w%d" % o][:, 0:TC + XC].indirect(T.inv[:, at // 16:(at + n) // 16]), "y%d%d" % (o, i))
+    for i, (at, n) in enumerate(YP):
+        for o in range(2):
+            sy.wait_ge(S["y%d%d" % (o, i)], 1)
+            sy.dma_start(T.y[:, TC * o + at:TC * o + at + n], T["y%d" % o][:, at:at + n]).then_inc(S.out, 16)
+    sy.wait_ge(S.out, 16 * 2 * len(YP))
+    g.wait_ge(S.sent, 2 * 2 * (N - 1))

@@ -3,26 +3,35 @@ from concourse.mybir import dt, AluOpType, ActivationFunctionType
 
 N, CAPP, XC, HC, TC = 8, 32, 256, 128, 512
 HALF = N // 2
-ARR = (N - 1) * CAPP
+NEAR = (HALF - 1) * CAPP
 VI = TC + 32
 VW = VI + 368
-FAR = 1024
-YP = ((0, 192), (192, 320))
-CALLS = ((False, (0,)), (False, (1,)), (True, (0, 1)))
-VSTEPS = "e0 e1 t x0 e2 e3 c00 x1 c02 o c10 c12 p00 p02 p10 h0 p12 h1"
-ASTEPS = "c01 c03 c11 c13 p01 p03 p11 p13 f j"
+FAR = 1024.0
+RAW = 0
+SNDR = 0
+LOADS = "s:x0 s:x1 a:s s:p s:w s:k0 s:k1"
+YG = (0, 96, 192, 352, 512, 768, 1024)
+YS = (0, 192, 512, 1024)
+CALLS = (((0, (0, 1, 2, 3)), (1, (0, 1, 2, 3))), ((0, (0, 1, 2)), (1, (0, 1, 2))))
+VSTEPS = "e0 e1 e2 e3 x0 t x1 c00 o0 c02 c10 c12 p00 p02 h0 i0 w i1 k0 h1 i2 k1 i3 u i4 i5 i6 i7 i8 a10 y0 y2 y4"
+ASTEPS = "v f c01 c03 c11 c13 p01 p03 p10 p11 p12 p13 j d00 d01 d10 d11 a00 a01 a11 y1 y3 y5"
+TSTEPS = "c00 c01 c02 c03 c10 c11 c12 c13 d00 d01 d10 d11 a00 a01 a10 a11"
+GSTEPS = "dg pc tab kneg jc"
 
 
 def _buffers():
     b = {}
-    for dtype, names in (("bfloat16", {"xb": 1024, "kb": 2048, "qb": 1024, "dg": 128, "ez": VI, "xd0": XC, "xd1": XC, "xd2": XC, "xd3": XC, "hb0": 512, "hb1": 512,
-                                       "vals": XC, "vl": VW, "tr": VI, "tab": 128, "tabt": 128}),
-                         ("int32", {"sl": 16, "pl": 16, "kneg": 16}),
-                         ("uint16", {"so": 16, "po": 16, "inv": 32, "eoff": 2}),
-                         ("float32", {"far": 1, "nk": 16, "pm": 16, "jc": 32, "jt": 32, "sf": 32, "w0": TC + XC, "w1": TC + XC, "y0": TC, "y1": TC})):
+    for dtype, names in (("bfloat16", {"xb": 1024, "kb": 2048, "qb": 1024, "dg": 128, "ez": VI, "rb0": 512, "rb1": 512, "hb0": 512, "hb1": 512,
+                                       "xd0": XC, "xd1": XC, "xd2": XC, "xd3": XC,
+                                       "vals": HC, "vl": VW, "tr": VI, "tab": 128, "tabt": 128}),
+                         ("int32", {"sl": 16, "pl": 8, "kneg": 8}),
+                         ("uint16", {"so": 64, "po": 8, "inv": 32, "eoff": 2}),
+                         ("float32", {"pc": 16, "nk": 8, "pm": 8, "sm": 32, "jc": 32, "jt": 32, "sf": 32, "w0": TC + XC + CAPP, "w1": TC + XC + CAPP,
+                                      "yb": 2 * TC})):
         for k, w in names.items():
             b[k] = ("sbuf", [128, w], dtype)
-    for q, s, w in (("eq", "es", 512), ("xq", "xs", XC), ("hq0", "hs0", HC), ("hq1", "hs1", HC), ("aq", "asc", ARR), ("kq", "ks", TC), ("wq", "ws", XC)):
+    for q, s, w in (("eq", "es", 512), ("xq0", "xs0", HC), ("xq1", "xs1", HC), ("aq", "asc", HC), ("hq", "hs", HC), ("bq", "bs", HC + 2 * NEAR),
+                    ("kq", "ks", TC), ("wq", "ws", XC)):
         b[q] = ("sbuf", [128, w], "float8_e4m3fn_x4")
         b[s] = ("sbuf", [128, w], "uint8")
     for p in ("pd0", "pd1", "pd2", "pd3", "py0", "py1", "py2", "py3"):
@@ -31,20 +40,23 @@ def _buffers():
 
 
 SCRATCH = _buffers()
-SEMAPHORES = ("lx0 lx1 lsnd lplc lqw lkc out arr sent dg far ez0 ez eq0 eq1 eq2 eq3 qx0 qx1 conv hq0 hq1 wq kq0 kq1 tab tabt eoff kneg vals jc jt vinit "
-              "ia ib ic ie it iu inv mo0 mo1 co0 co1 mk00 mk01 mk10 mk11 ck00 ck01 ck10 ck11 ma0 ma1 ca0 ca1 y00 y01 y10 y11 "
-              "m00 m01 m02 m03 m10 m11 m12 m13 c00 c01 c02 c03 c10 c11 c12 c13 g00 g01 g02 g03 g10 g11 g12 g13").split()
+SEMAPHORES = ("lx lx0 lx1 lsnd lplc lqw lk0 lk1 out arr0 arr1 sent dg pc ez0 ez tab kneg jc f v j t u w k0 k1 x0 x1 h0 h1 y0 y1 y2 y3 y4 y5 y6 y7 "
+              "e0 e1 e2 e3 r0 r1 o0 o1 o2 o3 i0 i1 i2 i3 i4 i5 i6 i7 i8 p00 p01 p02 p03 p10 p11 p12 p13 "
+              "c00 c01 c02 c03 c10 c11 c12 c13 d00 d01 d10 d11 a00 a01 a10 a11 "
+              "mc00 mc01 mc02 mc03 mc10 mc11 mc12 mc13 md00 md01 md10 md11 ma00 ma01 ma10 ma11").split()
 
 
-def send_masks(core, dests, topo):
-    near = [d for d in dests if topo.die(d) == topo.die(core)]
-    far = [d for d in dests if topo.die(d) != topo.die(core)]
-    masks = {}
-    for group, first in ((far, 0), (near, 1)):
-        for k, d in enumerate(group):
-            e = topo.engines(core, d)
-            masks[d] = (1 << e[4 * k + first]) | (1 << e[4 * k + first + 2])
-    return masks
+def landing(pos):
+    return 0 if 2 * pos < HALF else NEAR + HC
+
+
+def engines_of(e, part, planes, m):
+    even, odd = e[0::2], e[1::2]
+    if part == 0:
+        return (even, odd)[planes][2 * m:2 * m + 2]
+    if len(CALLS[1]) == 2:
+        return (odd[0:4], odd[4:8], even[4 * planes:4 * planes + 4])[m]
+    return ((odd[0:4], odd[4:8], even[0:4]), (e[0:8], e[8:16], even[4:8]))[planes][m]
 
 
 def rank_program(g, core, T, topo):
@@ -57,6 +69,13 @@ def rank_program(g, core, T, topo):
     A = AluOpType
     half, pos = rank // HALF, rank % HALF
     halves = (1 - half, half)
+    own = NEAR + CAPP * pos
+    b0, b1 = min(landing(pos), own), max(landing(pos) + NEAR, own + CAPP)
+    KC = HC + b1 - b0
+
+    def wait(q, names, n=1):
+        for s in names.split():
+            q.wait_ge(S[s], n)
 
     def copy(q, out, win, sem):
         if q is v:
@@ -64,179 +83,243 @@ def rank_program(g, core, T, topo):
         else:
             a.activation(out, win, COPY).then_inc(S[sem], 1)
 
-    for h in range(2):
-        sy.dma_start(T.xb[:, 512 * h:512 * h + 512], T.x[:, 512 * h:512 * h + 512]).then_inc(S["lx%d" % h], 16)
-    for k in range(8):
-        a.dma_start(T.sl[16 * k:16 * k + 16, :], T.snd[:, :]).then_inc(S.lsnd, 16)
-    for k in range(8):
-        sy.dma_start(T.pl[16 * k:16 * k + 16, :], T.plc[:, :]).then_inc(S.lplc, 16)
-    sy.dma_start(T.qb[:], T.qw[:, :]).then_inc(S.lqw, 16)
-    sy.dma_start(T.kb[:], T.kc[:, :]).then_inc(S.lkc, 16)
+    def dests(r, part):
+        return [d for d in range(N) if d != r and (d // HALF == r // HALF) == bool(part)]
 
-    g.iota(T.dg[:], [[-1, 128]], 0, 1, allow_small_or_imprecise_dtypes=True).then_inc(S.dg, 1)
+    def engines(r, d, planes):
+        part = int(d // HALF == r // HALF)
+        return engines_of(topo.engines(T.cores[r], T.cores[d]), part, planes, dests(r, part).index(d))
+
+    arrivals = [sum(len(engines(s, rank, p)) for s in dests(rank, part) for p in (0, 1)) for part in (0, 1)]
+    sent = sum(len(engines(rank, d, p)) for part in (0, 1) for d in dests(rank, part) for p in (0, 1))
+
+    for w in LOADS.split():
+        q, w = {"s": sy, "a": a}[w[0]], w[2:]
+        if w == "x":
+            q.dma_start(T.xb[:], T.x[:, :]).then_inc(S.lx, 16)
+        elif w == "w":
+            q.dma_start(T.qb[:], T.qw[:, :]).then_inc(S.lqw, 16)
+        elif w[0] == "x":
+            h = int(w[1])
+            q.dma_start(T.xb[:, 512 * h:512 * h + 512], T.x[:, 512 * h:512 * h + 512]).then_inc(S["lx%d" % h], 16)
+        elif w[0] == "k":
+            h = int(w[1])
+            q.dma_start(T.kb[:, 1024 * h:1024 * h + 1024], T.kc[:, 1024 * h:1024 * h + 1024]).then_inc(S["lk%d" % h], 16)
+        elif w[0] == "s":
+            for k in ([int(c) for c in w[1:]] or range(8)):
+                q.dma_start(T.sl[16 * k:16 * k + 16, :], T.snd[:, :]).then_inc(S.lsnd, 16)
+        else:
+            for k in ([int(c) for c in w[1:]] or range(8)):
+                q.dma_start(T.pl[16 * k:16 * k + 16, :], T.plc[:, 8 * (k // 4):8 * (k // 4) + 8]).then_inc(S.lplc, 16)
+
+    for w in GSTEPS.split():
+        if w == "dg":
+            g.iota(T.dg[:], [[-1, 128]], 0, 1, allow_small_or_imprecise_dtypes=True).then_inc(S.dg, 1)
+        elif w == "pc":
+            g.iota(T.pc[:], [[CAPP, 16]], -HC, 1, allow_small_or_imprecise_dtypes=True).then_inc(S.pc, 1)
+        elif w == "tab":
+            g.iota(T.tab[:, 0:64], [[256, 2], [-16, 2], [16, 16]], 16, 0, allow_small_or_imprecise_dtypes=True).then_inc(S.tab, 1)
+            g.iota(T.tab[:, 64:96], [[-16, 2], [0, 16]], 16, 0, allow_small_or_imprecise_dtypes=True).then_inc(S.tab, 1)
+            g.iota(T.tab[:, 96:128], [[0, 2], [1, 16]], 0, 0, allow_small_or_imprecise_dtypes=True).then_inc(S.tab, 1)
+        elif w == "kneg":
+            g.iota(T.kneg[:], [[-16, 8]], -VI, -1).then_inc(S.kneg, 1)
+        else:
+            g.iota(T.jc[:], [[16, 32]], KC - HC, 0, allow_small_or_imprecise_dtypes=True).then_inc(S.jc, 1)
     v.memset(T.ez[:], 0.0).then_inc(S.ez0, 1)
-    v.wait_ge(S.dg, 1)
-    v.wait_ge(S.ez0, 1)
+    wait(v, "dg ez0")
     v.tensor_scalar(T.ez[:, 3:515:4], T.dg[:], 0.0, None, A.is_equal).then_inc(S.ez, 1)
-    g.iota(T.tab[:, 0:64], [[256, 2], [-16, 2], [16, 16]], 16, 0, allow_small_or_imprecise_dtypes=True).then_inc(S.tab, 1)
-    g.iota(T.tab[:, 64:96], [[-16, 2], [0, 16]], 16, 0, allow_small_or_imprecise_dtypes=True).then_inc(S.tab, 1)
-    g.iota(T.tab[:, 96:128], [[0, 2], [1, 16]], 0, 0, allow_small_or_imprecise_dtypes=True).then_inc(S.tab, 1)
-    g.iota(T.far[:], [[0, 1]], FAR, 0, allow_small_or_imprecise_dtypes=True).then_inc(S.far, 1)
-    g.iota(T.jc[:], [[16, 32]], XC, 0, allow_small_or_imprecise_dtypes=True).then_inc(S.jc, 1)
-    g.iota(T.kneg[:], [[-16, 16]], -VI, -1).then_inc(S.kneg, 1)
-    nv = 0
-    for at, n, base in ((HC * halves[0], HC, 0), (HC * half, CAPP * pos, HC), (CAPP * rank, CAPP, ARR),
-                        (CAPP * rank + CAPP, HC - CAPP * pos - CAPP, HC + CAPP * pos)):
-        if n:
-            g.iota(T.vals[:, at:at + n], [[1, n]], base, 0, allow_small_or_imprecise_dtypes=True).then_inc(S.vals, 1)
-            nv += 1
 
-    def quant_e(b):
-        v.wait_ge(S.ez, 1)
-        v.quantize_mx(T.eq[:, 128 * b:128 * b + 128], T.es[:, 128 * b:128 * b + 128], T.ez[:, 3 - b:3 - b + 512]).then_inc(S["eq%d" % b], 1)
+    arrived = HC + landing(pos) - b0
+    runs = [r for r in ((HC * halves[0], HC, 0), (HC * half, CAPP * pos, arrived), (CAPP * rank, CAPP, HC + own - b0),
+                        (CAPP * rank + CAPP, NEAR - CAPP * pos, arrived + CAPP * pos)) if r[1]]
 
-    def quant_x(h):
-        v.wait_ge(S["lx%d" % h], 16)
-        v.quantize_mx(T.xq[:, HC * h:HC * h + HC], T.xs[:, HC * h:HC * h + HC],
-                      T.xb[:, 512 * h:512 * h + 512]).then_inc(S["qx%d" % h], 1)
+    def bank(w):
+        k, i, o = w[0], int(w[1]), int(w[2])
+        if RAW:
+            if k == "c":
+                return T["pd%d" % o], "" if i else "c1%d" % o
+            return T["py%d" % (2 * i + o)], "" if k == "d" else "d%d%d" % (i, o)
+        if k == "c":
+            return T[("pd%d", "py%d")[i] % o], ""
+        o += 2 * (k == "a")
+        return T[("pd%d", "py%d")[i] % o], "c%d%d" % (i, o)
 
-    def tables():
-        v.wait_ge(S.tab, 3)
-        v.transpose(T.tabt[:], T.tab[:]).then_inc(S.tabt, 1)
+    def step(q, w):
+        k, n = w[0], [int(c) for c in w[1:]]
+        if k == "e":
+            wait(v, "ez")
+            v.quantize_mx(T.eq[:, 128 * n[0]:128 * n[0] + 128], T.es[:, 128 * n[0]:128 * n[0] + 128], T.ez[:, 3 - n[0]:515 - n[0]]).then_inc(S[w], 1)
+        elif k == "r":
+            rows = 32 << n[0]
+            if n[0]:
+                wait(v, "r0")
+            else:
+                wait(v, "lsnd", 32)
+            v.tensor_copy(T.sl[rows:2 * rows, :], T.sl[0:rows, :]).then_inc(S[w], 1)
+        elif k == "o":
+            if SNDR:
+                wait(v, "r1")
+            else:
+                wait(v, "lsnd", 128)
+            if RAW:
+                v.tensor_scalar(T.so[:, 16 * n[0]:16 * n[0] + 16], T.sl[:], 4.0, float(n[0]), A.mult, A.add).then_inc(S[w], 1)
+            else:
+                v.tensor_copy(T.so[:, 0:16], T.sl[:]).then_inc(S[w], 1)
+        elif k == "p":
+            if RAW:
+                wait(q, "o%d" % n[1])
+                wait(q, "lx", 16)
+                c = 16 * n[1] + 2 * HALF * halves[n[0]]
+                copy(q, T["rb%d" % n[0]][:, n[1]:512:4], T.xb[:, 0:1024].indirect(T.so[:, c:c + 2 * HALF]), w)
+            else:
+                wait(q, "o0 c0%d c1%d" % (n[1], n[1]))
+                c = 2 * HALF * halves[n[0]]
+                copy(q, T["hb%d" % n[0]][:, n[1]:512:4], T["xd%d" % n[1]][:, 0:XC].indirect(T.so[:, c:c + 2 * HALF]), w)
+        elif k == "x":
+            if RAW:
+                wait(v, " ".join("p%d%d" % (n[0], b) for b in range(4)))
+                v.quantize_mx(T["xq%d" % n[0]][:], T["xs%d" % n[0]][:], T["rb%d" % n[0]][:]).then_inc(S[w], 1)
+            else:
+                wait(v, "l" + w, 16)
+                v.quantize_mx(T["xq%d" % n[0]][:], T["xs%d" % n[0]][:], T.xb[:, 512 * n[0]:512 * n[0] + 512]).then_inc(S[w], 1)
+        elif k == "c":
+            wait(q, "m" + w)
+            if RAW:
+                copy(q, T["hb%d" % n[0]][:, n[1]:512:4], bank(w)[0][:, 0:HC], w)
+            else:
+                copy(q, T["xd%d" % n[1]][:, HC * n[0]:HC * n[0] + HC], bank(w)[0][:, 0:HC], w)
+        elif k == "h":
+            wait(v, " ".join("%s%d%d" % ("pc"[RAW], n[0], b) for b in range(4)))
+            if n[0]:
+                v.quantize_mx(T.bq[:, NEAR:NEAR + HC], T.bs[:, NEAR:NEAR + HC], T.hb1[:]).then_inc(S[w], 1)
+            else:
+                v.quantize_mx(T.hq[:], T.hs[:], T.hb0[:]).then_inc(S[w], 1)
+        elif k == "w":
+            wait(v, "lqw", 16)
+            v.quantize_mx(T.wq[:], T.ws[:], T.qb[:]).then_inc(S[w], 1)
+        elif k == "k":
+            wait(v, "l" + w, 16)
+            v.quantize_mx(T.kq[:, 256 * n[0]:256 * n[0] + 256], T.ks[:, 256 * n[0]:256 * n[0] + 256],
+                          T.kb[:, 1024 * n[0]:1024 * n[0] + 1024]).then_inc(S[w], 1)
+        elif k == "d":
+            wait(q, "m" + w)
+            copy(q, T["w%d" % n[1]][:, KC + 256 * n[0]:KC + 256 * n[0] + 256], bank(w)[0][:, 0:256], w)
+        elif k == "a":
+            wait(q, "m" + w)
+            lo, hi = ((0, HC), (HC, KC))[n[0]]
+            copy(q, T["w%d" % n[1]][:, lo:hi], bank(w)[0][:, 0:hi - lo], w)
+        elif k == "t":
+            wait(v, "tab", 3)
+            v.transpose(T.tabt[:], T.tab[:]).then_inc(S[w], 1)
+        elif k == "u":
+            wait(v, "t")
+            v.tensor_copy(T.eoff[:], T.tabt[:, 0:64:32]).then_inc(S[w], 1)
+        elif k == "f":
+            if q is v:
+                v.memset(T.vl[:, 0:VI], FAR).then_inc(S[w], 1)
+            else:
+                wait(a, "ez")
+                a.activation(T.vl[:, 0:VI], T.ez[:], COPY, bias=FAR, scale=0.0).then_inc(S[w], 1)
+        elif k == "v":
+            wait(a, "dg pc")
+            for at, cnt, place in runs:
+                p, at = 64 * (at // HC), at % HC
+                a.activation(T.vals[p:p + 64, at:at + cnt], T.dg[p:p + 64, 0:cnt], IDENT, bias=T.pc[p:p + 64, place // CAPP:place // CAPP + 1],
+                             scale=-1.0).then_inc(S[w], 1)
+        elif k == "j":
+            wait(a, "t jc")
+            a.activation(T.jt[:], T.jc[:], IDENT, bias=T.tabt[:, 96:97]).then_inc(S[w], 1)
+        elif w == "i0":
+            wait(v, "kneg")
+            wait(v, "lplc", 128)
+            v.tensor_tensor(T.nk[:], T.pl[:], T.kneg[:], A.mult).then_inc(S[w], 1)
+        elif w == "i1":
+            wait(v, "i0")
+            v.tensor_tensor(T.pm[:], T.nk[:], T.pl[:], A.max).then_inc(S[w], 1)
+        elif w == "i2":
+            wait(v, "i1 t")
+            v.tensor_scalar(T.po[:], T.pm[:], T.tabt[:, 64:65], None, A.add).then_inc(S[w], 1)
+        elif w == "i3":
+            wait(v, "i2 f")
+            wait(v, "v", len(runs))
+            v.tensor_copy(T.vl[:, 0:VW].indirect(T.po[:, 0:8]), T.vals[:]).then_inc(S[w], 1)
+        elif w == "i4":
+            wait(v, "i3")
+            v.transpose(T.tr[:], T.vl[:, 0:VI]).then_inc(S[w], 1)
+        elif w == "i5":
+            wait(v, "i4 u j")
+            v.tensor_tensor(T.sf[:], T.tr[:, 0:VI].indirect(T.eoff[:, 0:2]), T.jt[:], A.min).then_inc(S[w], 1)
+        elif w == "i6":
+            wait(v, "i5")
+            v.tensor_tensor(T.sm[0:64, :], T.sf[0:64, :], T.sf[64:128, :], A.min).then_inc(S[w], 1)
+        elif k == "i":
+            wait(v, "i6")
+            p = 64 * (n[0] - 7)
+            v.tensor_scalar(T.inv[p:p + 64, :], T.sm[0:64, :], float(HC), None, A.add).then_inc(S[w], 1)
+        else:
+            lo, hi = YG[n[0]], YG[n[0] + 1]
+            o = lo // TC
+            wait(q, "i7 i8 d0%d d1%d a0%d a1%d" % (o, o, o, o))
+            copy(q, T.yb[:, lo:hi], T["w%d" % o][:, 0:KC + TC].indirect(T.inv[:, (lo - TC * o) // 16:(hi - TC * o) // 16]), w)
 
-    def unpack(q, h, b):
-        q.wait_ge(S["m%d%d" % (h, b)], 1)
-        copy(q, T["xd%d" % b][:, HC * h:HC * h + HC], T[("pd%d", "py%d")[h] % b][:, 0:HC], "c%d%d" % (h, b))
+    def product(w):
+        k, i, o = w[0], int(w[1]), int(w[2])
+        wait(t, bank(w)[1])
+        if k == "c":
+            if i or not RAW:
+                wait(t, "x%d e%d" % (i, o))
+                q, s, n = T["xq%d" % i][:], T["xs%d" % i][:], HC
+            else:
+                wait(t, "arr0", arrivals[0])
+                q, s, n = T.aq[:], T.asc[:], HC
+            lq, ls = T.eq, T.es
+        else:
+            wait(t, "w")
+            if k == "d":
+                wait(t, "k%d" % i)
+                q, s, n = T.kq[:, 256 * i:256 * i + 256], T.ks[:, 256 * i:256 * i + 256], 256
+            elif i:
+                wait(t, "arr1", arrivals[1])
+                wait(t, "h1")
+                q, s, n = T.bq[:, b0:b1], T.bs[:, b0:b1], b1 - b0
+            elif RAW:
+                wait(t, "h0")
+                q, s, n = T.hq[:], T.hs[:], HC
+            else:
+                wait(t, "arr0", arrivals[0])
+                q, s, n = T.aq[:], T.asc[:], HC
+            lq, ls = T.wq, T.ws
+        t.matmul_mx(bank(w)[0][:, 0:n], lq[:, 128 * o:128 * o + 128], ls[:, 128 * o:128 * o + 128], q, s, True, True).then_inc(S["m" + w], 1)
 
-    def offsets():
-        v.wait_ge(S.lsnd, 128)
-        v.tensor_copy(T.so[:], T.sl[:]).then_inc(S.conv, 1)
-
-    def pick(q, ph, b):
-        q.wait_ge(S.conv, 1)
-        q.wait_ge(S["c0%d" % b], 1)
-        q.wait_ge(S["c1%d" % b], 1)
-        c = 2 * HALF * halves[ph]
-        copy(q, T["hb%d" % ph][:, b:512:4], T["xd%d" % b][:, 0:XC].indirect(T.so[:, c:c + 2 * HALF]), "g%d%d" % (ph, b))
-
-    def quant_h(ph):
-        for b in range(4):
-            v.wait_ge(S["g%d%d" % (ph, b)], 1)
-        v.quantize_mx(T["hq%d" % ph][:], T["hs%d" % ph][:], T["hb%d" % ph][:]).then_inc(S["hq%d" % ph], 1)
-
-    for h in range(2):
-        t.wait_ge(S["qx%d" % h], 1)
-        for b in range(4):
-            t.wait_ge(S["eq%d" % b], 1)
-            t.matmul_mx(T[("pd%d", "py%d")[h] % b][:, 0:HC], T.eq[:, 128 * b:128 * b + 128], T.es[:, 128 * b:128 * b + 128],
-                        T.xq[:, HC * h:HC * h + HC], T.xs[:, HC * h:HC * h + HC], True, True).then_inc(S["m%d%d" % (h, b)], 1)
     for q, steps in ((v, VSTEPS), (a, ASTEPS)):
         for w in steps.split():
-            n = [int(c) for c in w[1:]]
-            if w[0] == "e":
-                quant_e(*n)
-            elif w[0] == "t":
-                tables()
-            elif w[0] == "x":
-                quant_x(*n)
-            elif w[0] == "c":
-                unpack(q, *n)
-            elif w[0] == "o":
-                offsets()
-            elif w[0] == "p":
-                pick(q, *n)
-            elif w[0] == "h":
-                quant_h(*n)
-            elif w[0] == "f":
-                a.wait_ge(S.far, 1)
-                a.wait_ge(S.ez, 1)
-                a.activation(T.vl[:, 0:VI], T.ez[:], IDENT, bias=T.far[:, 0:1], scale=0.0).then_inc(S.vinit, 1)
-            else:
-                a.wait_ge(S.tabt, 1)
-                a.wait_ge(S.jc, 1)
-                a.activation(T.jt[:], T.jc[:], IDENT, bias=T.tabt[:, 96:97]).then_inc(S.jt, 1)
+            step(q, w)
+    for w in TSTEPS.split():
+        product(w)
 
-    masks = send_masks(core, [c for c in T.cores if c != core], topo)
-    for planes, parts in CALLS:
-        tr = []
-        for ph in parts:
-            g.wait_ge(S["hq%d" % ph], 1)
-            for k in range(HALF):
-                d = HALF * halves[ph] + k
-                if d == rank:
-                    continue
-                dst = T.cores[d]
-                rid, pid = topo.addr(dst)[:2]
-                lo = CAPP * k
-                at = HC * ph + CAPP * (pos - (1 if ph and rank > d else 0))
-                if planes:
-                    src, out = T["hs%d" % ph][:, lo:lo + CAPP], T.asc[:, at:at + CAPP]
+    for part, ready in ((0, "x0" if RAW else "h0"), (1, "h1")):
+        wait(g, ready)
+        for planes, ms in CALLS[part]:
+            tr = []
+            for m in ms:
+                d = dests(rank, part)[m]
+                rid, pid = topo.addr(T.cores[d])[:2]
+                k = d % HALF
+                if part == 0:
+                    src, lo = ((T.xq0, T.xs0) if RAW else (T.hq, T.hs))[planes], CAPP * k
+                    out, at = (T.aq, T.asc)[planes], CAPP * pos
                 else:
-                    src, out = T["hq%d" % ph][:, lo:lo + CAPP].bitcast(dt.uint8), T.aq[:, at:at + CAPP].bitcast(dt.uint8)
-                tr.append(RemoteDMATransfer(dst_ids=[DstId(rid=rid, pnc=pid)], dma_engine_mask=masks[dst],
-                                            remote_sem=S.arr, srcs=[src], dsts=[out]))
-        g.remote_dma_fused(tr, local_sem=S.sent)
+                    src, lo = (T.bq, T.bs)[planes], NEAR + CAPP * k
+                    out, at = src, landing(k) + CAPP * (pos - (1 if pos > k else 0))
+                src, out = src[:, lo:lo + CAPP], out[:, at:at + CAPP]
+                if not planes:
+                    src, out = src.bitcast(dt.uint8), out.bitcast(dt.uint8)
+                tr.append(RemoteDMATransfer(dst_ids=[DstId(rid=rid, pnc=pid)], dma_engine_mask=sum(1 << e for e in engines(rank, d, planes)),
+                                            remote_sem=S["arr%d" % part], srcs=[src], dsts=[out]))
+            g.remote_dma_fused(tr, local_sem=S.sent)
 
-    v.wait_ge(S.lplc, 128)
-    v.wait_ge(S.kneg, 1)
-    v.tensor_tensor(T.nk[:], T.pl[:], T.kneg[:], A.mult).then_inc(S.ia, 1)
-    v.wait_ge(S.lqw, 16)
-    v.quantize_mx(T.wq[:], T.ws[:], T.qb[:]).then_inc(S.wq, 1)
-    v.wait_ge(S.ia, 1)
-    v.tensor_tensor(T.pm[:], T.nk[:], T.pl[:], A.max).then_inc(S.ib, 1)
-    v.wait_ge(S.lkc, 16)
-    v.quantize_mx(T.kq[:, 0:256], T.ks[:, 0:256], T.kb[:, 0:1024]).then_inc(S.kq0, 1)
-    v.wait_ge(S.ib, 1)
-    v.wait_ge(S.tabt, 1)
-    v.tensor_scalar(T.po[:], T.pm[:], T.tabt[:, 64:65], None, A.add).then_inc(S.ic, 1)
-    v.quantize_mx(T.kq[:, 256:512], T.ks[:, 256:512], T.kb[:, 1024:2048]).then_inc(S.kq1, 1)
-    v.wait_ge(S.ic, 1)
-    v.wait_ge(S.vals, nv)
-    v.wait_ge(S.vinit, 1)
-    v.tensor_copy(T.vl[:, 0:VW].indirect(T.po[:, 0:16]), T.vals[:, 0:XC]).then_inc(S.ie, 1)
-    v.tensor_copy(T.eoff[:], T.tabt[:, 0:64:32]).then_inc(S.eoff, 1)
-    v.wait_ge(S.ie, 1)
-    v.transpose(T.tr[:], T.vl[:, 0:VI]).then_inc(S.it, 1)
-    v.wait_ge(S.it, 1)
-    v.wait_ge(S.eoff, 1)
-    v.wait_ge(S.jt, 1)
-    v.tensor_tensor(T.sf[:], T.tr[:, 0:VI].indirect(T.eoff[:, 0:2]), T.jt[:], A.min).then_inc(S.iu, 1)
-    v.wait_ge(S.iu, 1)
-    v.tensor_copy(T.inv[:], T.sf[:]).then_inc(S.inv, 1)
-
-    def product(bank, o, q, s, n, sem):
-        t.matmul_mx(T[bank][:, 0:n], T.wq[:, 128 * o:128 * o + 128], T.ws[:, 128 * o:128 * o + 128], q, s, True, True).then_inc(S[sem], 1)
-    t.wait_ge(S.wq, 1)
-    for h, bank in ((0, "py%d"), (1, "pd%d")):
-        t.wait_ge(S["kq%d" % h], 1)
-        for o in range(2):
-            t.wait_ge(S["c%d%d" % (1 - h, o)], 1)
-            product(bank % o, o, T.kq[:, 256 * h:256 * h + 256], T.ks[:, 256 * h:256 * h + 256], 256, "mk%d%d" % (h, o))
-            a.wait_ge(S["mk%d%d" % (h, o)], 1)
-            copy(a, T["w%d" % o][:, XC + 256 * h:XC + 256 * h + 256], T[bank % o][:, 0:256], "ck%d%d" % (h, o))
-    for o in range(2):
-        bank = "py%d" % (2 + o)
-        t.wait_ge(S["c1%d" % (2 + o)], 1)
-        product(bank, o, T.hq1[:], T.hs1[:], HC, "mo%d" % o)
-        a.wait_ge(S["mo%d" % o], 1)
-        copy(a, T["w%d" % o][:, ARR:XC], T[bank][:, CAPP * pos:CAPP * pos + CAPP], "co%d" % o)
-
-    t.wait_ge(S.arr, 2 * 2 * (N - 1))
-    for o in range(2):
-        t.wait_ge(S["c0%d" % (2 + o)], 1)
-        product("pd%d" % (2 + o), o, T.aq[:], T.asc[:], ARR, "ma%d" % o)
-
-    for o, q in ((0, v), (1, a)):
-        q.wait_ge(S["ma%d" % o], 1)
-        copy(q, T["w%d" % o][:, 0:ARR], T["pd%d" % (2 + o)][:, 0:ARR], "ca%d" % o)
-        for s in ("co%d", "ck0%d", "ck1%d", "ca%d"):
-            q.wait_ge(S[s % o], 1)
-        q.wait_ge(S.inv, 1)
-        for i, (at, n) in enumerate(YP):
-            copy(q, T["y%d" % o][:, at:at + n], T["w%d" % o][:, 0:TC + XC].indirect(T.inv[:, at // 16:(at + n) // 16]), "y%d%d" % (o, i))
-    for i, (at, n) in enumerate(YP):
-        for o in range(2):
-            sy.wait_ge(S["y%d%d" % (o, i)], 1)
-            sy.dma_start(T.y[:, TC * o + at:TC * o + at + n], T["y%d" % o][:, at:at + n]).then_inc(S.out, 16)
-    sy.wait_ge(S.out, 16 * 2 * len(YP))
-    g.wait_ge(S.sent, 2 * 2 * (N - 1))
+    for lo, hi in zip(YS, YS[1:]):
+        wait(sy, " ".join("y%d" % i for i in range(len(YG) - 1) if lo <= YG[i] < hi))
+        sy.dma_start(T.y[:, lo:hi], T.yb[:, lo:hi]).then_inc(S.out, 16)
+    wait(sy, "out", 16 * (len(YS) - 1))
+    wait(g, "sent", sent)

@@ -3,35 +3,39 @@ from concourse.mybir import dt, AluOpType, ActivationFunctionType
 
 N, CAPP, XC, HC, TC = 8, 32, 256, 128, 512
 HALF = N // 2
-NEAR = (HALF - 1) * CAPP
 VI = TC + 32
 VW = VI + 368
 FAR = 1024.0
-RAW = 0
-SNDR = 0
-LOADS = "s:x0 s:x1 a:s s:p s:w s:k0 s:k1"
-YG = (0, 96, 192, 352, 512, 768, 1024)
-YS = (0, 192, 512, 1024)
-CALLS = (((0, (0, 1, 2, 3)), (1, (0, 1, 2, 3))), ((0, (0, 1, 2)), (1, (0, 1, 2))))
-VSTEPS = "e0 e1 e2 e3 x0 t x1 c00 o0 c02 c10 c12 p00 p02 h0 i0 w i1 k0 h1 i2 k1 i3 u i4 i5 i6 i7 i8 a10 y0 y2 y4"
-ASTEPS = "v f c01 c03 c11 c13 p01 p03 p10 p11 p12 p13 j d00 d01 d10 d11 a00 a01 a11 y1 y3 y5"
-TSTEPS = "c00 c01 c02 c03 c10 c11 c12 c13 d00 d01 d10 d11 a00 a01 a10 a11"
-GSTEPS = "dg pc tab kneg jc"
+PARTS = ((1,), (2, 3, 4, 5), (6, 7, 8))
+UNP = 4 * CAPP
+FIRST = (0, 384, 288)
+TILE = (0, 384, 256)
+LATE = CAPP * len(PARTS[2])
+CALLS = ((0, 0, ((1, (1, 3)),)),
+         (0, 1, ((1, (0, 2)),)),
+         (1, 0, ((2, (0,)), (3, (1,)), (4, (2,)), (5, (3,)))),
+         (1, 1, ((2, (0,)), (3, (1,)), (4, (3,)), (5, (2,)))),
+         (2, 0, ((6, (0, 1)), (7, (2, 3)))),
+         (2, 1, ((6, (0, 1)), (7, (2, 3)))))
+YG = (0, 160, 320, 512, 704, 864, 1024)
+YS = (0, 320, 704, 1024)
+VSTEPS = "z0 z1 e0 e1 x0 e3 e2 x1 o0 o1 o2 t i0 c02 c10 c12 p00 p02 i1 h0 p10 p12 i2 h1 w k0 h2 k1 i3 u i4 i5 i6 i7 i8 a10 y0 y2 y4"
+ASTEPS = "f c00 c01 c03 c11 c13 p01 p03 p11 p13 p20 p21 p22 p23 j d00 d01 d10 d11 a00 a01 a11 y1 y3 y5"
+TSTEPS = "c00 c01 c03 c02 c11 c10 c13 c12 d00 d01 d10 d11 a00 a01 a10 a11"
+GSTEPS = "dg tab kneg jc v0 v1"
 
 
 def _buffers():
     b = {}
-    for dtype, names in (("bfloat16", {"xb": 1024, "kb": 2048, "qb": 1024, "dg": 128, "ez": VI, "rb0": 512, "rb1": 512, "hb0": 512, "hb1": 512,
-                                       "xd0": XC, "xd1": XC, "xd2": XC, "xd3": XC,
+    for dtype, names in (("bfloat16", {"xb": 1024, "kb": 2048, "qb": 1024, "dg": 128, "ez": VI, "hb": 2048,
                                        "vals": HC, "vl": VW, "tr": VI, "tab": 128, "tabt": 128}),
                          ("int32", {"sl": 16, "pl": 8, "kneg": 8}),
-                         ("uint16", {"so": 64, "po": 8, "inv": 32, "eoff": 2}),
-                         ("float32", {"pc": 16, "nk": 8, "pm": 8, "sm": 32, "jc": 32, "jt": 32, "sf": 32, "w0": TC + XC + CAPP, "w1": TC + XC + CAPP,
-                                      "yb": 2 * TC})):
+                         ("uint16", {"so": 16, "po": 8, "inv": 32, "eoff": 2}),
+                         ("float32", {"nk": 8, "pm": 8, "sm": 32, "jc": 32, "jt": 32, "sf": 32, "w0": XC + TC, "w1": XC + TC, "yb": 2 * TC})):
         for k, w in names.items():
             b[k] = ("sbuf", [128, w], dtype)
-    for q, s, w in (("eq", "es", 512), ("xq0", "xs0", HC), ("xq1", "xs1", HC), ("aq", "asc", HC), ("hq", "hs", HC), ("bq", "bs", HC + 2 * NEAR),
-                    ("kq", "ks", TC), ("wq", "ws", XC)):
+    for q, s, w in (("eq", "es", 512), ("xq0", "xs0", HC), ("xq1", "xs1", HC), ("hq0", "hs0", HC), ("hq1", "hs1", HC), ("hq2", "hs2", HC + LATE - CAPP),
+                    ("aq", "asc", XC - LATE), ("kq", "ks", TC), ("wq", "ws", XC)):
         b[q] = ("sbuf", [128, w], "float8_e4m3fn_x4")
         b[s] = ("sbuf", [128, w], "uint8")
     for p in ("pd0", "pd1", "pd2", "pd3", "py0", "py1", "py2", "py3"):
@@ -40,23 +44,16 @@ def _buffers():
 
 
 SCRATCH = _buffers()
-SEMAPHORES = ("lx lx0 lx1 lsnd lplc lqw lk0 lk1 out arr0 arr1 sent dg pc ez0 ez tab kneg jc f v j t u w k0 k1 x0 x1 h0 h1 y0 y1 y2 y3 y4 y5 y6 y7 "
-              "e0 e1 e2 e3 r0 r1 o0 o1 o2 o3 i0 i1 i2 i3 i4 i5 i6 i7 i8 p00 p01 p02 p03 p10 p11 p12 p13 "
-              "c00 c01 c02 c03 c10 c11 c12 c13 d00 d01 d10 d11 a00 a01 a10 a11 "
-              "mc00 mc01 mc02 mc03 mc10 mc11 mc12 mc13 md00 md01 md10 md11 ma00 ma01 ma10 ma11").split()
+SEMAPHORES = "lx0 lx1 lsnd lplc lqw lk0 lk1 out arr0 arr1 sent vec act ten gps".split()
 
 
-def landing(pos):
-    return 0 if 2 * pos < HALF else NEAR + HC
+def destinations(r):
+    base = r - r % HALF
+    return [(base + HALF + k) % N for k in range(HALF)] + [base + (r + k) % HALF for k in range(1, HALF + 1)]
 
 
-def engines_of(e, part, planes, m):
-    even, odd = e[0::2], e[1::2]
-    if part == 0:
-        return (even, odd)[planes][2 * m:2 * m + 2]
-    if len(CALLS[1]) == 2:
-        return (odd[0:4], odd[4:8], even[4 * planes:4 * planes + 4])[m]
-    return ((odd[0:4], odd[4:8], even[0:4]), (e[0:8], e[8:16], even[4:8]))[planes][m]
+def place(s, r):
+    return CAPP * ((s - r) % HALF if s // HALF == r // HALF else HALF + s % HALF)
 
 
 def rank_program(g, core, T, topo):
@@ -67,259 +64,201 @@ def rank_program(g, core, T, topo):
     v, a, t, sy = g.vector, g.scalar, g.tensor, g.sync
     COPY, IDENT = ActivationFunctionType.Copy, ActivationFunctionType.Identity
     A = AluOpType
-    half, pos = rank // HALF, rank % HALF
-    halves = (1 - half, half)
-    own = NEAR + CAPP * pos
-    b0, b1 = min(landing(pos), own), max(landing(pos) + NEAR, own + CAPP)
-    KC = HC + b1 - b0
+    order = destinations(rank)
+    pos = rank % HALF
+    cuts = (0, HALF, N - 1 - (pos if pos < HALF - 1 else 1), N)
 
-    def wait(q, names, n=1):
-        for s in names.split():
-            q.wait_ge(S[s], n)
+    done = {"l" + w: ("l" + w, 16) for w in ("x0", "x1", "qw", "k0", "k1")}
+    done.update({"lsnd": ("lsnd", 128), "lplc": ("lplc", 128), "out": ("out", 16 * (len(YS) - 1))})
+    writes = [(d, 4 * len(groups)) for _, _, tr in CALLS for d, groups in tr]
+    for late in (0, 1):
+        done["arr%d" % late] = ("arr%d" % late, sum(n for s in range(N) for d, n in writes if destinations(s)[d - 1] == rank and (d in PARTS[2]) == late))
+    done["sent"] = ("sent", sum(n for _, n in writes))
+    for sem, mark, steps in (("vec", "", VSTEPS), ("act", "", ASTEPS), ("ten", "m", TSTEPS), ("gps", "", GSTEPS)):
+        done.update({mark + w: (sem, i + 1) for i, w in enumerate(steps.split())})
+    seen = {}
 
-    def copy(q, out, win, sem):
-        if q is v:
-            v.tensor_copy(out, win).then_inc(S[sem], 1)
-        else:
-            a.activation(out, win, COPY).then_inc(S[sem], 1)
+    def wait(queue, names):
+        q, need = {"vec": v, "act": a, "ten": t, "gps": g, "syn": sy}[queue], {}
+        for w in names.split():
+            sem, n = done[w]
+            need[sem] = max(need.get(sem, 0), n)
+        for sem, n in need.items():
+            if seen.get((queue, sem), 0) < n:
+                q.wait_ge(S[sem], n)
+                seen[queue, sem] = n
 
-    def dests(r, part):
-        return [d for d in range(N) if d != r and (d // HALF == r // HALF) == bool(part)]
+    def copy(queue, out, win):
+        return v.tensor_copy(out, win) if queue == "vec" else a.activation(out, win, COPY)
 
-    def engines(r, d, planes):
-        part = int(d // HALF == r // HALF)
-        return engines_of(topo.engines(T.cores[r], T.cores[d]), part, planes, dests(r, part).index(d))
+    for h in range(2):
+        sy.dma_start(T.xb[:, 512 * h:512 * h + 512], T.x[:, 512 * h:512 * h + 512]).then_inc(S["lx%d" % h], 16)
+    for k in range(8):
+        a.dma_start(T.sl[16 * k:16 * k + 16, :], T.snd[:, :]).then_inc(S.lsnd, 16)
+    for k in range(8):
+        sy.dma_start(T.pl[16 * k:16 * k + 16, :], T.plc[:, 8 * (k // 4):8 * (k // 4) + 8]).then_inc(S.lplc, 16)
+    sy.dma_start(T.qb[:], T.qw[:, :]).then_inc(S.lqw, 16)
+    for h in range(2):
+        sy.dma_start(T.kb[:, 1024 * h:1024 * h + 1024], T.kc[:, 1024 * h:1024 * h + 1024]).then_inc(S["lk%d" % h], 16)
 
-    arrivals = [sum(len(engines(s, rank, p)) for s in dests(rank, part) for p in (0, 1)) for part in (0, 1)]
-    sent = sum(len(engines(rank, d, p)) for part in (0, 1) for d in dests(rank, part) for p in (0, 1))
-
-    for w in LOADS.split():
-        q, w = {"s": sy, "a": a}[w[0]], w[2:]
-        if w == "x":
-            q.dma_start(T.xb[:], T.x[:, :]).then_inc(S.lx, 16)
-        elif w == "w":
-            q.dma_start(T.qb[:], T.qw[:, :]).then_inc(S.lqw, 16)
-        elif w[0] == "x":
-            h = int(w[1])
-            q.dma_start(T.xb[:, 512 * h:512 * h + 512], T.x[:, 512 * h:512 * h + 512]).then_inc(S["lx%d" % h], 16)
-        elif w[0] == "k":
-            h = int(w[1])
-            q.dma_start(T.kb[:, 1024 * h:1024 * h + 1024], T.kc[:, 1024 * h:1024 * h + 1024]).then_inc(S["lk%d" % h], 16)
-        elif w[0] == "s":
-            for k in ([int(c) for c in w[1:]] or range(8)):
-                q.dma_start(T.sl[16 * k:16 * k + 16, :], T.snd[:, :]).then_inc(S.lsnd, 16)
-        else:
-            for k in ([int(c) for c in w[1:]] or range(8)):
-                q.dma_start(T.pl[16 * k:16 * k + 16, :], T.plc[:, 8 * (k // 4):8 * (k // 4) + 8]).then_inc(S.lplc, 16)
-
-    for w in GSTEPS.split():
+    def count(w):
         if w == "dg":
-            g.iota(T.dg[:], [[-1, 128]], 0, 1, allow_small_or_imprecise_dtypes=True).then_inc(S.dg, 1)
-        elif w == "pc":
-            g.iota(T.pc[:], [[CAPP, 16]], -HC, 1, allow_small_or_imprecise_dtypes=True).then_inc(S.pc, 1)
-        elif w == "tab":
-            g.iota(T.tab[:, 0:64], [[256, 2], [-16, 2], [16, 16]], 16, 0, allow_small_or_imprecise_dtypes=True).then_inc(S.tab, 1)
-            g.iota(T.tab[:, 64:96], [[-16, 2], [0, 16]], 16, 0, allow_small_or_imprecise_dtypes=True).then_inc(S.tab, 1)
-            g.iota(T.tab[:, 96:128], [[0, 2], [1, 16]], 0, 0, allow_small_or_imprecise_dtypes=True).then_inc(S.tab, 1)
-        elif w == "kneg":
-            g.iota(T.kneg[:], [[-16, 8]], -VI, -1).then_inc(S.kneg, 1)
-        else:
-            g.iota(T.jc[:], [[16, 32]], KC - HC, 0, allow_small_or_imprecise_dtypes=True).then_inc(S.jc, 1)
-    v.memset(T.ez[:], 0.0).then_inc(S.ez0, 1)
-    wait(v, "dg ez0")
-    v.tensor_scalar(T.ez[:, 3:515:4], T.dg[:], 0.0, None, A.is_equal).then_inc(S.ez, 1)
-
-    arrived = HC + landing(pos) - b0
-    runs = [r for r in ((HC * halves[0], HC, 0), (HC * half, CAPP * pos, arrived), (CAPP * rank, CAPP, HC + own - b0),
-                        (CAPP * rank + CAPP, NEAR - CAPP * pos, arrived + CAPP * pos)) if r[1]]
+            return g.iota(T.dg[:], [[-1, 128]], 0, 1, allow_small_or_imprecise_dtypes=True)
+        if w[0] == "v":
+            h = int(w[1])
+            if h:
+                wait("gps", "v0")
+            cuts = sorted({HC * h, min(max(CAPP * rank, HC * h), HC * h + HC), HC * h + HC})
+            for lo, hi in zip(cuts, cuts[1:]):
+                last = g.iota(T.vals[64 * h:64 * h + 64, lo - HC * h:hi - HC * h], [[1, hi - lo]], place(lo // CAPP, rank), 0,
+                              allow_small_or_imprecise_dtypes=True)
+            return last
+        if w == "tab":
+            g.iota(T.tab[:, 0:64], [[256, 2], [-16, 2], [16, 16]], 16, 0, allow_small_or_imprecise_dtypes=True)
+            g.iota(T.tab[:, 64:96], [[-16, 2], [0, 16]], 16, 0, allow_small_or_imprecise_dtypes=True)
+            return g.iota(T.tab[:, 96:128], [[0, 2], [1, 16]], 0, 0, allow_small_or_imprecise_dtypes=True)
+        if w == "kneg":
+            return g.iota(T.kneg[:], [[-16, 8]], -VI, -1)
+        return g.iota(T.jc[:], [[16, 32]], XC, 0, allow_small_or_imprecise_dtypes=True)
 
     def bank(w):
         k, i, o = w[0], int(w[1]), int(w[2])
-        if RAW:
-            if k == "c":
-                return T["pd%d" % o], "" if i else "c1%d" % o
-            return T["py%d" % (2 * i + o)], "" if k == "d" else "d%d%d" % (i, o)
-        if k == "c":
-            return T[("pd%d", "py%d")[i] % o], ""
-        o += 2 * (k == "a")
-        return T[("pd%d", "py%d")[i] % o], "c%d%d" % (i, o)
+        return T[("pd%d", "py%d")[i] % (o + 2 * (k == "a"))]
 
     def step(q, w):
         k, n = w[0], [int(c) for c in w[1:]]
+        if w == "z0":
+            return v.memset(T.ez[:], 0.0)
+        if w == "z1":
+            wait(q, "dg z0")
+            return v.tensor_scalar(T.ez[:, 3:515:4], T.dg[:], 0.0, None, A.is_equal)
         if k == "e":
-            wait(v, "ez")
-            v.quantize_mx(T.eq[:, 128 * n[0]:128 * n[0] + 128], T.es[:, 128 * n[0]:128 * n[0] + 128], T.ez[:, 3 - n[0]:515 - n[0]]).then_inc(S[w], 1)
-        elif k == "r":
-            rows = 32 << n[0]
+            wait(q, "z1")
+            return v.quantize_mx(T.eq[:, 128 * n[0]:128 * n[0] + 128], T.es[:, 128 * n[0]:128 * n[0] + 128], T.ez[:, 3 - n[0]:515 - n[0]])
+        if k == "o":
+            wait(q, "lsnd")
+            lo, hi = cuts[n[0]], cuts[n[0] + 1]
+            return v.tensor_copy(T.so[:, 2 * lo:2 * hi], T.sl[:, 2 * order[lo]:2 * (order[lo] + hi - lo)])
+        if k == "p":
+            wait(q, "o0 c0%d c1%d" % (n[1], n[1]) + ("", " o1", " o1 o2")[n[0]])
+            d, at, win = PARTS[n[0]], 4 * FIRST[n[0]], UNP + XC * n[1]
+            return copy(q, T.hb[:, at + n[1]:at + 4 * CAPP * len(d):4], T.hb[:, win:win + XC].indirect(T.so[:, 2 * d[0] - 2:2 * d[-1]]))
+        if k == "x":
+            wait(q, "l" + w)
+            return v.quantize_mx(T["xq%d" % n[0]][:], T["xs%d" % n[0]][:], T.xb[:, 512 * n[0]:512 * n[0] + 512])
+        if k == "c":
+            wait(q, "m" + w)
+            at = UNP + XC * n[1] + HC * n[0]
+            return copy(q, T.hb[:, at:at + HC], bank(w)[:, 0:HC])
+        if k == "h":
+            wait(q, " ".join("p%d%d" % (n[0], b) for b in range(4)))
+            return v.quantize_mx(T["hq%d" % n[0]][:, 0:HC], T["hs%d" % n[0]][:, 0:HC], T.hb[:, 4 * TILE[n[0]]:4 * TILE[n[0]] + 512])
+        if k == "w":
+            wait(q, "lqw")
+            return v.quantize_mx(T.wq[:], T.ws[:], T.qb[:])
+        if k == "k":
+            wait(q, "l" + w)
+            return v.quantize_mx(T.kq[:, 256 * n[0]:256 * n[0] + 256], T.ks[:, 256 * n[0]:256 * n[0] + 256], T.kb[:, 1024 * n[0]:1024 * n[0] + 1024])
+        if k == "d":
+            wait(q, "m" + w)
+            return copy(q, T["w%d" % n[1]][:, XC + 256 * n[0]:XC + 256 * n[0] + 256], bank(w)[:, 0:256])
+        if k == "a":
+            wait(q, "m" + w)
             if n[0]:
-                wait(v, "r0")
-            else:
-                wait(v, "lsnd", 32)
-            v.tensor_copy(T.sl[rows:2 * rows, :], T.sl[0:rows, :]).then_inc(S[w], 1)
-        elif k == "o":
-            if SNDR:
-                wait(v, "r1")
-            else:
-                wait(v, "lsnd", 128)
-            if RAW:
-                v.tensor_scalar(T.so[:, 16 * n[0]:16 * n[0] + 16], T.sl[:], 4.0, float(n[0]), A.mult, A.add).then_inc(S[w], 1)
-            else:
-                v.tensor_copy(T.so[:, 0:16], T.sl[:]).then_inc(S[w], 1)
-        elif k == "p":
-            if RAW:
-                wait(q, "o%d" % n[1])
-                wait(q, "lx", 16)
-                c = 16 * n[1] + 2 * HALF * halves[n[0]]
-                copy(q, T["rb%d" % n[0]][:, n[1]:512:4], T.xb[:, 0:1024].indirect(T.so[:, c:c + 2 * HALF]), w)
-            else:
-                wait(q, "o0 c0%d c1%d" % (n[1], n[1]))
-                c = 2 * HALF * halves[n[0]]
-                copy(q, T["hb%d" % n[0]][:, n[1]:512:4], T["xd%d" % n[1]][:, 0:XC].indirect(T.so[:, c:c + 2 * HALF]), w)
-        elif k == "x":
-            if RAW:
-                wait(v, " ".join("p%d%d" % (n[0], b) for b in range(4)))
-                v.quantize_mx(T["xq%d" % n[0]][:], T["xs%d" % n[0]][:], T["rb%d" % n[0]][:]).then_inc(S[w], 1)
-            else:
-                wait(v, "l" + w, 16)
-                v.quantize_mx(T["xq%d" % n[0]][:], T["xs%d" % n[0]][:], T.xb[:, 512 * n[0]:512 * n[0] + 512]).then_inc(S[w], 1)
-        elif k == "c":
-            wait(q, "m" + w)
-            if RAW:
-                copy(q, T["hb%d" % n[0]][:, n[1]:512:4], bank(w)[0][:, 0:HC], w)
-            else:
-                copy(q, T["xd%d" % n[1]][:, HC * n[0]:HC * n[0] + HC], bank(w)[0][:, 0:HC], w)
-        elif k == "h":
-            wait(v, " ".join("%s%d%d" % ("pc"[RAW], n[0], b) for b in range(4)))
-            if n[0]:
-                v.quantize_mx(T.bq[:, NEAR:NEAR + HC], T.bs[:, NEAR:NEAR + HC], T.hb1[:]).then_inc(S[w], 1)
-            else:
-                v.quantize_mx(T.hq[:], T.hs[:], T.hb0[:]).then_inc(S[w], 1)
-        elif k == "w":
-            wait(v, "lqw", 16)
-            v.quantize_mx(T.wq[:], T.ws[:], T.qb[:]).then_inc(S[w], 1)
-        elif k == "k":
-            wait(v, "l" + w, 16)
-            v.quantize_mx(T.kq[:, 256 * n[0]:256 * n[0] + 256], T.ks[:, 256 * n[0]:256 * n[0] + 256],
-                          T.kb[:, 1024 * n[0]:1024 * n[0] + 1024]).then_inc(S[w], 1)
-        elif k == "d":
-            wait(q, "m" + w)
-            copy(q, T["w%d" % n[1]][:, KC + 256 * n[0]:KC + 256 * n[0] + 256], bank(w)[0][:, 0:256], w)
-        elif k == "a":
-            wait(q, "m" + w)
-            lo, hi = ((0, HC), (HC, KC))[n[0]]
-            copy(q, T["w%d" % n[1]][:, lo:hi], bank(w)[0][:, 0:hi - lo], w)
-        elif k == "t":
-            wait(v, "tab", 3)
-            v.transpose(T.tabt[:], T.tab[:]).then_inc(S[w], 1)
-        elif k == "u":
-            wait(v, "t")
-            v.tensor_copy(T.eoff[:], T.tabt[:, 0:64:32]).then_inc(S[w], 1)
-        elif k == "f":
-            if q is v:
-                v.memset(T.vl[:, 0:VI], FAR).then_inc(S[w], 1)
-            else:
-                wait(a, "ez")
-                a.activation(T.vl[:, 0:VI], T.ez[:], COPY, bias=FAR, scale=0.0).then_inc(S[w], 1)
-        elif k == "v":
-            wait(a, "dg pc")
-            for at, cnt, place in runs:
-                p, at = 64 * (at // HC), at % HC
-                a.activation(T.vals[p:p + 64, at:at + cnt], T.dg[p:p + 64, 0:cnt], IDENT, bias=T.pc[p:p + 64, place // CAPP:place // CAPP + 1],
-                             scale=-1.0).then_inc(S[w], 1)
-        elif k == "j":
-            wait(a, "t jc")
-            a.activation(T.jt[:], T.jc[:], IDENT, bias=T.tabt[:, 96:97]).then_inc(S[w], 1)
-        elif w == "i0":
-            wait(v, "kneg")
-            wait(v, "lplc", 128)
-            v.tensor_tensor(T.nk[:], T.pl[:], T.kneg[:], A.mult).then_inc(S[w], 1)
-        elif w == "i1":
-            wait(v, "i0")
-            v.tensor_tensor(T.pm[:], T.nk[:], T.pl[:], A.max).then_inc(S[w], 1)
-        elif w == "i2":
-            wait(v, "i1 t")
-            v.tensor_scalar(T.po[:], T.pm[:], T.tabt[:, 64:65], None, A.add).then_inc(S[w], 1)
-        elif w == "i3":
-            wait(v, "i2 f")
-            wait(v, "v", len(runs))
-            v.tensor_copy(T.vl[:, 0:VW].indirect(T.po[:, 0:8]), T.vals[:]).then_inc(S[w], 1)
-        elif w == "i4":
-            wait(v, "i3")
-            v.transpose(T.tr[:], T.vl[:, 0:VI]).then_inc(S[w], 1)
-        elif w == "i5":
-            wait(v, "i4 u j")
-            v.tensor_tensor(T.sf[:], T.tr[:, 0:VI].indirect(T.eoff[:, 0:2]), T.jt[:], A.min).then_inc(S[w], 1)
-        elif w == "i6":
-            wait(v, "i5")
-            v.tensor_tensor(T.sm[0:64, :], T.sf[0:64, :], T.sf[64:128, :], A.min).then_inc(S[w], 1)
-        elif k == "i":
-            wait(v, "i6")
+                return copy(q, T["w%d" % n[1]][:, 0:LATE], bank(w)[:, HC - LATE:HC])
+            return copy(q, T["w%d" % n[1]][:, LATE:XC], bank(w)[:, 0:XC - LATE])
+        if k == "t":
+            wait(q, "tab")
+            return v.transpose(T.tabt[:], T.tab[:])
+        if k == "u":
+            wait(q, "t")
+            return v.tensor_copy(T.eoff[:], T.tabt[:, 0:64:32])
+        if k == "f":
+            wait(q, "z1")
+            return a.activation(T.vl[:, 0:VI], T.ez[:], COPY, bias=FAR, scale=0.0)
+        if k == "j":
+            wait(q, "t jc")
+            return a.activation(T.jt[:], T.jc[:], IDENT, bias=T.tabt[:, 96:97])
+        if w == "i0":
+            wait(q, "kneg lplc")
+            return v.tensor_tensor(T.nk[:], T.pl[:], T.kneg[:], A.mult)
+        if w == "i1":
+            wait(q, "i0")
+            return v.tensor_tensor(T.pm[:], T.nk[:], T.pl[:], A.max)
+        if w == "i2":
+            wait(q, "i1 t")
+            return v.tensor_scalar(T.po[:], T.pm[:], T.tabt[:, 64:65], None, A.add)
+        if w == "i3":
+            wait(q, "i2 f v1")
+            return v.tensor_copy(T.vl[:, 0:VW].indirect(T.po[:, 0:8]), T.vals[:])
+        if w == "i4":
+            wait(q, "i3")
+            return v.transpose(T.tr[:], T.vl[:, 0:VI])
+        if w == "i5":
+            wait(q, "i4 u j")
+            return v.tensor_tensor(T.sf[:], T.tr[:, 0:VI].indirect(T.eoff[:, 0:2]), T.jt[:], A.min)
+        if w == "i6":
+            wait(q, "i5")
+            return v.tensor_tensor(T.sm[0:64, :], T.sf[0:64, :], T.sf[64:128, :], A.min)
+        if k == "i":
+            wait(q, "i6")
             p = 64 * (n[0] - 7)
-            v.tensor_scalar(T.inv[p:p + 64, :], T.sm[0:64, :], float(HC), None, A.add).then_inc(S[w], 1)
-        else:
-            lo, hi = YG[n[0]], YG[n[0] + 1]
-            o = lo // TC
-            wait(q, "i7 i8 d0%d d1%d a0%d a1%d" % (o, o, o, o))
-            copy(q, T.yb[:, lo:hi], T["w%d" % o][:, 0:KC + TC].indirect(T.inv[:, (lo - TC * o) // 16:(hi - TC * o) // 16]), w)
+            return v.tensor_copy(T.inv[p:p + 64, :], T.sm[0:64, :])
+        lo, hi = YG[n[0]], YG[n[0] + 1]
+        o = lo // TC
+        wait(q, "i7 i8 d0%d d1%d a0%d a1%d" % (o, o, o, o))
+        return copy(q, T.yb[:, lo:hi], T["w%d" % o][:, 0:XC + TC].indirect(T.inv[:, (lo - TC * o) // 16:(hi - TC * o) // 16]))
 
     def product(w):
         k, i, o = w[0], int(w[1]), int(w[2])
-        wait(t, bank(w)[1])
+        lq, ls = T.wq, T.ws
         if k == "c":
-            if i or not RAW:
-                wait(t, "x%d e%d" % (i, o))
-                q, s, n = T["xq%d" % i][:], T["xs%d" % i][:], HC
-            else:
-                wait(t, "arr0", arrivals[0])
-                q, s, n = T.aq[:], T.asc[:], HC
+            wait("ten", "x%d e%d" % (i, o))
+            q, s, n = T["xq%d" % i][:], T["xs%d" % i][:], HC
             lq, ls = T.eq, T.es
+        elif k == "d":
+            wait("ten", "w k%d c%d%d" % (i, i, o))
+            q, s, n = T.kq[:, 256 * i:256 * i + 256], T.ks[:, 256 * i:256 * i + 256], 256
+        elif i:
+            wait("ten", "w h2 c1%d arr1" % (o + 2))
+            q, s, n = T.hq2[:, LATE - CAPP:], T.hs2[:, LATE - CAPP:], HC
         else:
-            wait(t, "w")
-            if k == "d":
-                wait(t, "k%d" % i)
-                q, s, n = T.kq[:, 256 * i:256 * i + 256], T.ks[:, 256 * i:256 * i + 256], 256
-            elif i:
-                wait(t, "arr1", arrivals[1])
-                wait(t, "h1")
-                q, s, n = T.bq[:, b0:b1], T.bs[:, b0:b1], b1 - b0
-            elif RAW:
-                wait(t, "h0")
-                q, s, n = T.hq[:], T.hs[:], HC
-            else:
-                wait(t, "arr0", arrivals[0])
-                q, s, n = T.aq[:], T.asc[:], HC
-            lq, ls = T.wq, T.ws
-        t.matmul_mx(bank(w)[0][:, 0:n], lq[:, 128 * o:128 * o + 128], ls[:, 128 * o:128 * o + 128], q, s, True, True).then_inc(S["m" + w], 1)
+            wait("ten", "w c0%d arr0" % (o + 2))
+            q, s, n = T.aq[:], T.asc[:], XC - LATE
+        return t.matmul_mx(bank(w)[:, 0:n], lq[:, 128 * o:128 * o + 128], ls[:, 128 * o:128 * o + 128], q, s, True, True)
 
-    for q, steps in ((v, VSTEPS), (a, ASTEPS)):
+    for w in GSTEPS.split():
+        count(w).then_inc(S.gps, 1)
+    for q, steps in (("vec", VSTEPS), ("act", ASTEPS)):
         for w in steps.split():
-            step(q, w)
+            step(q, w).then_inc(S[q], 1)
     for w in TSTEPS.split():
-        product(w)
+        product(w).then_inc(S.ten, 1)
 
-    for part, ready in ((0, "x0" if RAW else "h0"), (1, "h1")):
-        wait(g, ready)
-        for planes, ms in CALLS[part]:
-            tr = []
-            for m in ms:
-                d = dests(rank, part)[m]
-                rid, pid = topo.addr(T.cores[d])[:2]
-                k = d % HALF
-                if part == 0:
-                    src, lo = ((T.xq0, T.xs0) if RAW else (T.hq, T.hs))[planes], CAPP * k
-                    out, at = (T.aq, T.asc)[planes], CAPP * pos
-                else:
-                    src, lo = (T.bq, T.bs)[planes], NEAR + CAPP * k
-                    out, at = src, landing(k) + CAPP * (pos - (1 if pos > k else 0))
-                src, out = src[:, lo:lo + CAPP], out[:, at:at + CAPP]
-                if not planes:
-                    src, out = src.bitcast(dt.uint8), out.bitcast(dt.uint8)
-                tr.append(RemoteDMATransfer(dst_ids=[DstId(rid=rid, pnc=pid)], dma_engine_mask=sum(1 << e for e in engines(rank, d, planes)),
-                                            remote_sem=S["arr%d" % part], srcs=[src], dsts=[out]))
-            g.remote_dma_fused(tr, local_sem=S.sent)
+    for ready, planes, transfers in CALLS:
+        wait("gps", "h%d" % ready)
+        tr = []
+        for d, groups in transfers:
+            dst = T.cores[order[d - 1]]
+            rid, pid = topo.addr(dst)[:2]
+            part = [d in p for p in PARTS].index(True)
+            lo = FIRST[part] - TILE[part] + CAPP * (d - PARTS[part][0])
+            at = place(rank, order[d - 1])
+            src = T[("hq%d", "hs%d")[planes] % part][:, lo:lo + CAPP]
+            if part == 2:
+                out = (T.hq2, T.hs2)[planes][:, HC - CAPP + at:HC + at]
+            else:
+                out = (T.aq, T.asc)[planes][:, at - LATE:at - LATE + CAPP]
+            if not planes:
+                src, out = src.bitcast(dt.uint8), out.bitcast(dt.uint8)
+            eng = topo.engines(core, dst)
+            eng = eng[0::2] + eng[1::2]
+            tr.append(RemoteDMATransfer(dst_ids=[DstId(rid=rid, pnc=pid)], dma_engine_mask=sum(1 << e for k in groups for e in eng[4 * k:4 * k + 4]),
+                                        remote_sem=S["arr%d" % (part == 2)], srcs=[src], dsts=[out]))
+        g.remote_dma_fused(tr, local_sem=S.sent)
 
     for lo, hi in zip(YS, YS[1:]):
-        wait(sy, " ".join("y%d" % i for i in range(len(YG) - 1) if lo <= YG[i] < hi))
+        wait("syn", " ".join("y%d" % i for i in range(len(YG) - 1) if lo <= YG[i] < hi))
         sy.dma_start(T.y[:, lo:hi], T.yb[:, lo:hi]).then_inc(S.out, 16)
-    wait(sy, "out", 16 * (len(YS) - 1))
-    wait(g, "sent", sent)
+    wait("syn", "out")
+    wait("gps", "sent")

from concourse.bass import DstId, RemoteDMATransfer
from concourse.mybir import dt, AluOpType, ActivationFunctionType

N, CAPP, XC, HC, TC = 8, 32, 256, 128, 512
HALF = N // 2
VI = TC + 32
VW = VI + 368
FAR = 1024.0
PARTS = ((1,), (2, 3, 4, 5), (6, 7, 8))
UNP = 4 * CAPP
FIRST = (0, 384, 288)
TILE = (0, 384, 256)
LATE = CAPP * len(PARTS[2])
CALLS = ((0, 0, ((1, (1, 3)),)),
         (0, 1, ((1, (0, 2)),)),
         (1, 0, ((2, (0,)), (3, (1,)), (4, (2,)), (5, (3,)))),
         (1, 1, ((2, (0,)), (3, (1,)), (4, (3,)), (5, (2,)))),
         (2, 0, ((6, (0, 1)), (7, (2, 3)))),
         (2, 1, ((6, (0, 1)), (7, (2, 3)))))
YG = (0, 160, 320, 512, 704, 864, 1024)
YS = (0, 320, 704, 1024)
VSTEPS = "z0 z1 e0 e1 x0 e3 e2 x1 o0 o1 o2 t i0 c02 c10 c12 p00 p02 i1 h0 p10 p12 i2 h1 w k0 h2 k1 i3 u i4 i5 i6 i7 i8 a10 y0 y2 y4"
ASTEPS = "f c00 c01 c03 c11 c13 p01 p03 p11 p13 p20 p21 p22 p23 j d00 d01 d10 d11 a00 a01 a11 y1 y3 y5"
TSTEPS = "c00 c01 c03 c02 c11 c10 c13 c12 d00 d01 d10 d11 a00 a01 a10 a11"
GSTEPS = "dg tab kneg jc v0 v1"


def _buffers():
    b = {}
    for dtype, names in (("bfloat16", {"xb": 1024, "kb": 2048, "qb": 1024, "dg": 128, "ez": VI, "hb": 2048,
                                       "vals": HC, "vl": VW, "tr": VI, "tab": 128, "tabt": 128}),
                         ("int32", {"sl": 16, "pl": 8, "kneg": 8}),
                         ("uint16", {"so": 16, "po": 8, "inv": 32, "eoff": 2}),
                         ("float32", {"nk": 8, "pm": 8, "sm": 32, "jc": 32, "jt": 32, "sf": 32, "w0": XC + TC, "w1": XC + TC, "yb": 2 * TC})):
        for k, w in names.items():
            b[k] = ("sbuf", [128, w], dtype)
    for q, s, w in (("eq", "es", 512), ("xq0", "xs0", HC), ("xq1", "xs1", HC), ("hq0", "hs0", HC), ("hq1", "hs1", HC), ("hq2", "hs2", HC + LATE - CAPP),
                    ("aq", "asc", XC - LATE), ("kq", "ks", TC), ("wq", "ws", XC)):
        b[q] = ("sbuf", [128, w], "float8_e4m3fn_x4")
        b[s] = ("sbuf", [128, w], "uint8")
    for p in ("pd0", "pd1", "pd2", "pd3", "py0", "py1", "py2", "py3"):
        b[p] = ("psum", [128, 512], "float32")
    return b


SCRATCH = _buffers()
SEMAPHORES = "lx0 lx1 lsnd lplc lqw lk0 lk1 out arr0 arr1 sent vec act ten gps".split()


def destinations(r):
    base = r - r % HALF
    return [(base + HALF + k) % N for k in range(HALF)] + [base + (r + k) % HALF for k in range(1, HALF + 1)]


def place(s, r):
    return CAPP * ((s - r) % HALF if s // HALF == r // HALF else HALF + s % HALF)


def rank_program(g, core, T, topo):
    rank = T.rank_of(core)
    if rank is None:
        return
    S = T.sem
    v, a, t, sy = g.vector, g.scalar, g.tensor, g.sync
    COPY, IDENT = ActivationFunctionType.Copy, ActivationFunctionType.Identity
    A = AluOpType
    order = destinations(rank)
    pos = rank % HALF
    cuts = (0, HALF, N - 1 - (pos if pos < HALF - 1 else 1), N)

    done = {"l" + w: ("l" + w, 16) for w in ("x0", "x1", "qw", "k0", "k1")}
    done.update({"lsnd": ("lsnd", 128), "lplc": ("lplc", 128), "out": ("out", 16 * (len(YS) - 1))})
    writes = [(d, 4 * len(groups)) for _, _, tr in CALLS for d, groups in tr]
    for late in (0, 1):
        done["arr%d" % late] = ("arr%d" % late, sum(n for s in range(N) for d, n in writes if destinations(s)[d - 1] == rank and (d in PARTS[2]) == late))
    done["sent"] = ("sent", sum(n for _, n in writes))
    for sem, mark, steps in (("vec", "", VSTEPS), ("act", "", ASTEPS), ("ten", "m", TSTEPS), ("gps", "", GSTEPS)):
        done.update({mark + w: (sem, i + 1) for i, w in enumerate(steps.split())})
    seen = {}

    def wait(queue, names):
        q, need = {"vec": v, "act": a, "ten": t, "gps": g, "syn": sy}[queue], {}
        for w in names.split():
            sem, n = done[w]
            need[sem] = max(need.get(sem, 0), n)
        for sem, n in need.items():
            if seen.get((queue, sem), 0) < n:
                q.wait_ge(S[sem], n)
                seen[queue, sem] = n

    def copy(queue, out, win):
        return v.tensor_copy(out, win) if queue == "vec" else a.activation(out, win, COPY)

    for h in range(2):
        sy.dma_start(T.xb[:, 512 * h:512 * h + 512], T.x[:, 512 * h:512 * h + 512]).then_inc(S["lx%d" % h], 16)
    for k in range(8):
        a.dma_start(T.sl[16 * k:16 * k + 16, :], T.snd[:, :]).then_inc(S.lsnd, 16)
    for k in range(8):
        sy.dma_start(T.pl[16 * k:16 * k + 16, :], T.plc[:, 8 * (k // 4):8 * (k // 4) + 8]).then_inc(S.lplc, 16)
    sy.dma_start(T.qb[:], T.qw[:, :]).then_inc(S.lqw, 16)
    for h in range(2):
        sy.dma_start(T.kb[:, 1024 * h:1024 * h + 1024], T.kc[:, 1024 * h:1024 * h + 1024]).then_inc(S["lk%d" % h], 16)

    def count(w):
        if w == "dg":
            return g.iota(T.dg[:], [[-1, 128]], 0, 1, allow_small_or_imprecise_dtypes=True)
        if w[0] == "v":
            h = int(w[1])
            if h:
                wait("gps", "v0")
            cuts = sorted({HC * h, min(max(CAPP * rank, HC * h), HC * h + HC), HC * h + HC})
            for lo, hi in zip(cuts, cuts[1:]):
                last = g.iota(T.vals[64 * h:64 * h + 64, lo - HC * h:hi - HC * h], [[1, hi - lo]], place(lo // CAPP, rank), 0,
                              allow_small_or_imprecise_dtypes=True)
            return last
        if w == "tab":
            g.iota(T.tab[:, 0:64], [[256, 2], [-16, 2], [16, 16]], 16, 0, allow_small_or_imprecise_dtypes=True)
            g.iota(T.tab[:, 64:96], [[-16, 2], [0, 16]], 16, 0, allow_small_or_imprecise_dtypes=True)
            return g.iota(T.tab[:, 96:128], [[0, 2], [1, 16]], 0, 0, allow_small_or_imprecise_dtypes=True)
        if w == "kneg":
            return g.iota(T.kneg[:], [[-16, 8]], -VI, -1)
        return g.iota(T.jc[:], [[16, 32]], XC, 0, allow_small_or_imprecise_dtypes=True)

    def bank(w):
        k, i, o = w[0], int(w[1]), int(w[2])
        return T[("pd%d", "py%d")[i] % (o + 2 * (k == "a"))]

    def step(q, w):
        k, n = w[0], [int(c) for c in w[1:]]
        if w == "z0":
            return v.memset(T.ez[:], 0.0)
        if w == "z1":
            wait(q, "dg z0")
            return v.tensor_scalar(T.ez[:, 3:515:4], T.dg[:], 0.0, None, A.is_equal)
        if k == "e":
            wait(q, "z1")
            return v.quantize_mx(T.eq[:, 128 * n[0]:128 * n[0] + 128], T.es[:, 128 * n[0]:128 * n[0] + 128], T.ez[:, 3 - n[0]:515 - n[0]])
        if k == "o":
            wait(q, "lsnd")
            lo, hi = cuts[n[0]], cuts[n[0] + 1]
            return v.tensor_copy(T.so[:, 2 * lo:2 * hi], T.sl[:, 2 * order[lo]:2 * (order[lo] + hi - lo)])
        if k == "p":
            wait(q, "o0 c0%d c1%d" % (n[1], n[1]) + ("", " o1", " o1 o2")[n[0]])
            d, at, win = PARTS[n[0]], 4 * FIRST[n[0]], UNP + XC * n[1]
            return copy(q, T.hb[:, at + n[1]:at + 4 * CAPP * len(d):4], T.hb[:, win:win + XC].indirect(T.so[:, 2 * d[0] - 2:2 * d[-1]]))
        if k == "x":
            wait(q, "l" + w)
            return v.quantize_mx(T["xq%d" % n[0]][:], T["xs%d" % n[0]][:], T.xb[:, 512 * n[0]:512 * n[0] + 512])
        if k == "c":
            wait(q, "m" + w)
            at = UNP + XC * n[1] + HC * n[0]
            return copy(q, T.hb[:, at:at + HC], bank(w)[:, 0:HC])
        if k == "h":
            wait(q, " ".join("p%d%d" % (n[0], b) for b in range(4)))
            return v.quantize_mx(T["hq%d" % n[0]][:, 0:HC], T["hs%d" % n[0]][:, 0:HC], T.hb[:, 4 * TILE[n[0]]:4 * TILE[n[0]] + 512])
        if k == "w":
            wait(q, "lqw")
            return v.quantize_mx(T.wq[:], T.ws[:], T.qb[:])
        if k == "k":
            wait(q, "l" + w)
            return v.quantize_mx(T.kq[:, 256 * n[0]:256 * n[0] + 256], T.ks[:, 256 * n[0]:256 * n[0] + 256], T.kb[:, 1024 * n[0]:1024 * n[0] + 1024])
        if k == "d":
            wait(q, "m" + w)
            return copy(q, T["w%d" % n[1]][:, XC + 256 * n[0]:XC + 256 * n[0] + 256], bank(w)[:, 0:256])
        if k == "a":
            wait(q, "m" + w)
            if n[0]:
                return copy(q, T["w%d" % n[1]][:, 0:LATE], bank(w)[:, HC - LATE:HC])
            return copy(q, T["w%d" % n[1]][:, LATE:XC], bank(w)[:, 0:XC - LATE])
        if k == "t":
            wait(q, "tab")
            return v.transpose(T.tabt[:], T.tab[:])
        if k == "u":
            wait(q, "t")
            return v.tensor_copy(T.eoff[:], T.tabt[:, 0:64:32])
        if k == "f":
            wait(q, "z1")
            return a.activation(T.vl[:, 0:VI], T.ez[:], COPY, bias=FAR, scale=0.0)
        if k == "j":
            wait(q, "t jc")
            return a.activation(T.jt[:], T.jc[:], IDENT, bias=T.tabt[:, 96:97])
        if w == "i0":
            wait(q, "kneg lplc")
            return v.tensor_tensor(T.nk[:], T.pl[:], T.kneg[:], A.mult)
        if w == "i1":
            wait(q, "i0")
            return v.tensor_tensor(T.pm[:], T.nk[:], T.pl[:], A.max)
        if w == "i2":
            wait(q, "i1 t")
            return v.tensor_scalar(T.po[:], T.pm[:], T.tabt[:, 64:65], None, A.add)
        if w == "i3":
            wait(q, "i2 f v1")
            return v.tensor_copy(T.vl[:, 0:VW].indirect(T.po[:, 0:8]), T.vals[:])
        if w == "i4":
            wait(q, "i3")
            return v.transpose(T.tr[:], T.vl[:, 0:VI])
        if w == "i5":
            wait(q, "i4 u j")
            return v.tensor_tensor(T.sf[:], T.tr[:, 0:VI].indirect(T.eoff[:, 0:2]), T.jt[:], A.min)
        if w == "i6":
            wait(q, "i5")
            return v.tensor_tensor(T.sm[0:64, :], T.sf[0:64, :], T.sf[64:128, :], A.min)
        if k == "i":
            wait(q, "i6")
            p = 64 * (n[0] - 7)
            return v.tensor_copy(T.inv[p:p + 64, :], T.sm[0:64, :])
        lo, hi = YG[n[0]], YG[n[0] + 1]
        o = lo // TC
        wait(q, "i7 i8 d0%d d1%d a0%d a1%d" % (o, o, o, o))
        return copy(q, T.yb[:, lo:hi], T["w%d" % o][:, 0:XC + TC].indirect(T.inv[:, (lo - TC * o) // 16:(hi - TC * o) // 16]))

    def product(w):
        k, i, o = w[0], int(w[1]), int(w[2])
        lq, ls = T.wq, T.ws
        if k == "c":
            wait("ten", "x%d e%d" % (i, o))
            q, s, n = T["xq%d" % i][:], T["xs%d" % i][:], HC
            lq, ls = T.eq, T.es
        elif k == "d":
            wait("ten", "w k%d c%d%d" % (i, i, o))
            q, s, n = T.kq[:, 256 * i:256 * i + 256], T.ks[:, 256 * i:256 * i + 256], 256
        elif i:
            wait("ten", "w h2 c1%d arr1" % (o + 2))
            q, s, n = T.hq2[:, LATE - CAPP:], T.hs2[:, LATE - CAPP:], HC
        else:
            wait("ten", "w c0%d arr0" % (o + 2))
            q, s, n = T.aq[:], T.asc[:], XC - LATE
        return t.matmul_mx(bank(w)[:, 0:n], lq[:, 128 * o:128 * o + 128], ls[:, 128 * o:128 * o + 128], q, s, True, True)

    for w in GSTEPS.split():
        count(w).then_inc(S.gps, 1)
    for q, steps in (("vec", VSTEPS), ("act", ASTEPS)):
        for w in steps.split():
            step(q, w).then_inc(S[q], 1)
    for w in TSTEPS.split():
        product(w).then_inc(S.ten, 1)

    for ready, planes, transfers in CALLS:
        wait("gps", "h%d" % ready)
        tr = []
        for d, groups in transfers:
            dst = T.cores[order[d - 1]]
            rid, pid = topo.addr(dst)[:2]
            part = [d in p for p in PARTS].index(True)
            lo = FIRST[part] - TILE[part] + CAPP * (d - PARTS[part][0])
            at = place(rank, order[d - 1])
            src = T[("hq%d", "hs%d")[planes] % part][:, lo:lo + CAPP]
            if part == 2:
                out = (T.hq2, T.hs2)[planes][:, HC - CAPP + at:HC + at]
            else:
                out = (T.aq, T.asc)[planes][:, at - LATE:at - LATE + CAPP]
            if not planes:
                src, out = src.bitcast(dt.uint8), out.bitcast(dt.uint8)
            eng = topo.engines(core, dst)
            eng = eng[0::2] + eng[1::2]
            tr.append(RemoteDMATransfer(dst_ids=[DstId(rid=rid, pnc=pid)], dma_engine_mask=sum(1 << e for k in groups for e in eng[4 * k:4 * k + 4]),
                                        remote_sem=S["arr%d" % (part == 2)], srcs=[src], dsts=[out]))
        g.remote_dma_fused(tr, local_sem=S.sent)

    for lo, hi in zip(YS, YS[1:]):
        wait("syn", " ".join("y%d" % i for i in range(len(YG) - 1) if lo <= YG[i] < hi))
        sy.dma_start(T.y[:, lo:hi], T.yb[:, lo:hi]).then_inc(S.out, 16)
    wait("syn", "out")
    wait("gps", "sent")
